import numpy as np, ml_dtypes
CORES = [2,3,42,43,82,83,122,123]
N = 8
BF = ml_dtypes.bfloat16
def gentries(a):
    return np.ascontiguousarray(a.reshape(8, 16, -1).transpose(0, 2, 1)).reshape(8, -1)
def gtable(e):
    e = np.asarray(e); return np.ascontiguousarray(e.reshape(8, -1, 16).transpose(0, 2, 1)).reshape(128, -1).astype(np.int32)
W, S, J, RO, LW = 4096, 8, 512, 8, 12
K = S * J
def pack(x, p, c):
    return {"ring": np.ascontiguousarray(x.reshape(N, 128, W)).astype(np.float32).astype(BF), "place": np.stack([gtable(a.reshape(8, K)) for a in p]),
            "carry": np.ascontiguousarray(c.reshape(N, 128, J)).astype(np.float32).astype(BF)}
def parts(rng):
    return rng.integers(0, 16, (N, 8, 16, W)), rng.integers(0, W, (N, 8, J, S)), rng.integers(0, 16, (N, 8, 16, J))
def extremes(rng, n):
    m = rng.integers(0, 4, (N, 8, 1, n))
    return np.where(m == 0, 0, np.where(m == 1, 15, 15 * rng.integers(0, 2, (N, 8, 16, n))))
def single(rng, hit):
    dig = rng.integers(0, 16, hit.shape)
    return (hit & (np.arange(16)[:, None] == dig)).astype(np.int64)
def setup_inputs(rng):
    x, p, c = parts(rng)
    return pack(x, p, c)
def setup_inputs_spread(rng):
    top = rng.choice(np.array([0, 1, 3, 7, 15]), (N, 8, 1, W)); x = ((top + 1) * rng.random((N, 8, 16, W))).astype(np.int64)
    top = rng.choice(np.array([0, 1, 3, 7, 15]), (N, 8, 1, J)); c = ((top + 1) * rng.random((N, 8, 16, J))).astype(np.int64)
    wd = 2 ** rng.integers(0, LW + 1, (N, 8, J, 1))
    p = (rng.integers(0, W, (N, 8, J, 1)) + (wd * rng.random((N, 8, J, S))).astype(np.int64)) & (W - 1)
    x[..., 5::16] = 15; x[..., 6::16] = 0; x[..., 7::16] = 8; h = 16 * rng.integers(0, W // 16, (N, 8, J, S))
    for j, a in ((0, 15), (2, 14), (J - 3, 14), (J - 1, 15)):
        c[:, :, :, j] = a; p[:, :, j] = h[:, :, j] + 5
    for j in (1, J - 2):
        c[:, :, :, j] = 0; p[:, :, j] = h[:, :, j] + 6; p[:, :, j, 0] += 1; p[:, :, j, S - 1] += 1
    return pack(x, p, c)
def setup_inputs_ends(rng):
    x = extremes(rng, W); c = extremes(rng, J); m = rng.integers(0, 4, (N, 8, J, 1))
    p = (W - 1) * np.where(m == 0, 0, np.where(m == 1, 1, rng.integers(0, 2, (N, 8, J, S))))
    x[:, 1::2, :, W - 1] = 15; x[:, 1::2, :, 0] = 0; x[:, 0::4, :, W - 1] = 0; x[:, 0::4, :, 0] = 15
    for j in (0, 3, J - 1):
        c[:, :, :, j] = 15; p[:, 1::2, j] = W - 1; p[:, 0::4, j] = 0
    for j in (1, 4, J - 2):
        c[:, :, :, j] = 0; p[:, 1::2, j] = 0; p[:, 0::4, j] = W - 1
    return pack(x, p, c)
def setup_inputs_corners(rng):
    x, p, c = parts(rng); run = np.arange(K).reshape(J, S) & (W - 1)
    for q in range(N):
        for g, m in enumerate(rng.permutation(8)):
            a = int(rng.integers(0, W))
            if m == 0: p[q, g] = a
            elif m == 1: p[q, g] = W - 1; c[q, g] = 15
            elif m == 2: p[q, g] = 0; c[q, g] = 0
            elif m == 3:
                p[q, g] = a; p[q, g, rng.integers(0, J), rng.integers(0, S)] = (a + 1 + rng.integers(0, W - 1)) & (W - 1)
            elif m == 4: p[q, g] = run
            elif m == 5: p[q, g] = W - 1 - run
            elif m == 6:
                x[q, g] = 0; x[q, g, :, W - 1] = 15; p[q, g] = rng.integers(-4, 4, (J, S)) & (W - 1)
            else:
                x[q, g] = 15; c[q, g, :, J - 1] = 15; c[q, g, :, J - 2] = 0
                s = np.add.reduce(c[q, g], axis=0); p[q, g, :, 0] = (W - s - (np.arange(J) & 1)) & (W - 1)
    return pack(x, p, c)
def setup_inputs_calm(rng):
    hit = rng.random((N, 8, 1, W)) < rng.choice(np.array([0.002, 0.008, 0.02]), (N, 8, 1, 1)); hit[..., :32] = False; hit[..., W - 8:] = False
    x = single(rng, hit); c = single(rng, rng.random((N, 8, 1, J)) < 0.25) * rng.integers(1, 4, (N, 8, 1, J))
    p = np.where(rng.random((N, 8, J, S)) < 0.5, rng.integers(-4, 4, (N, 8, J, S)) & (W - 1), rng.integers(0, W, (N, 8, J, S)))
    q = int(rng.integers(0, N)); g = int(rng.integers(0, 8)); c[q, g] = 0
    for t in range(RO):
        x[q, g] = 0; q = (q + 1 + t % (N - 1)) % N; g = (g + 1) % 8
    return pack(x, p, c)
def setup_inputs_full(rng):
    hit = rng.random((N, 8, 1, W)) < 0.004; top = 14 if S == 8 else 15
    for b in (0, 1): hit[..., (W - 1 - b + 240 * np.arange(-RO, RO + 1)) & (W - 1)] = False
    hit[:, 1::2, :, 15::16] = False
    x = single(rng, hit); x[:, 0::2] = 15 * x[:, 0::2]; x[:, 1::2] = top - x[:, 1::2]
    c = 15 - single(rng, rng.random((N, 8, 1, J)) < 0.125)
    late = (W - 1 - rng.integers(0, 2, (N, 8, J, S)) - 240 * rng.integers(0, RO, (N, 8, J, S))) & (W - 1)
    p = np.where(rng.random((N, 8, J, S)) < 0.5, late, rng.integers(0, W, (N, 8, J, S)))
    e = (W - 1 + 240 * (RO - 1)) & (W - 1); x[:, 0::2, :, e] = 7; x[:, 1::2, :, e] = 3
    c[:, :, :, J - 1] = 15; p[:, 1::2, J - 1] = W - 1; p[:, 0::2, J - 1] = late[:, 0::2, J - 1]; p[:, 0::2, J - 1, 0] = W - 1; p[:, 0::2, J - 1, S - 1] = W - 1
    return pack(x, p, c)
def check_inputs(d):
    bad = []
    for k, lo, hi in (("ring", 0, 15), ("place", 0, W - 1), ("carry", 0, 15)):
        a = np.asarray(d[k]).astype(np.float64)
        if not (np.min(a) >= lo and np.max(a) <= hi): bad.append("range of " + k)
        if np.any(a != np.floor(a)): bad.append("whole numbers in " + k)
    return bad
def reference(ring, place, carry):
    x = ring.astype(np.float32).astype(np.int32).reshape(N, 8, 16, W); c = carry.astype(np.float32).astype(np.int32).reshape(N, 8, 16, J)
    p = np.stack([gentries(a) for a in place]).astype(np.int64); shown = []
    for t in range(RO):
        v = np.take_along_axis(x, p[:, :, None, :], 3).reshape(N, 8, 16, J, S)
        after = (c[..., None] + np.add.accumulate(v, axis=4, dtype=np.int32)) & 15
        into = np.concatenate([c[..., None], after[..., :S - 1]], axis=4)
        p = (p + np.add.reduce(into, axis=2).reshape(N, 8, K)) & (W - 1)
        end = np.ascontiguousarray(after[..., S - 1]); shown.append(end.reshape(N, 128, J))
        c = np.roll(end, (1 + t % (N - 1), 1), axis=(0, 1))
    return {"yp": np.stack([gtable(a) for a in p]).astype(np.float32), "yc": np.concatenate(shown, axis=2).astype(np.float32).astype(BF)}

@@ -1,0 +1,415 @@
+from concourse.mybir import AluOpType as ALU, ActivationFunctionType as ACT
+
+W, S, J, RO = 4096, 8, 512, 8
+NCH = 4
+JC = J // NCH
+CC = JC * S // 16
+EC = JC * S
+MOVE = 240
+WX = W + MOVE * (RO - 1)
+NI = RO * NCH
+M = 3072.0
+BIAS = -32.0
+MID = 2048.0
+DRIFT = 8.0
+VSHARE = [384, 320, 448, 352] + [352, 320, 320, 320] * 6 + [384, 352, 320, 256]
+EXACT = [False, False, False, False]
+ADD_BY_SCAN = True
+
+SCRATCH = {
+    "win": ("sbuf", [128, WX], "bfloat16"),
+    "pl": ("sbuf", [128, 256], "int32"),
+    "plf": ("sbuf", [128, 256], "float16"),
+    "off": ("sbuf", [128, 256], "uint16"),
+    "land": ("sbuf", [128, RO * J], "bfloat16"),
+    "outc": ("sbuf", [128, RO * J], "bfloat16"),
+    "outy": ("sbuf", [128, RO * J], "bfloat16"),
+    "d1": ("sbuf", [128, J * S], "bfloat16"),
+    "fo": ("sbuf", [128, J * S], "bfloat16"),
+    "vv": ("sbuf", [128, J * S], "bfloat16"),
+    "de": ("sbuf", [128, J * S], "bfloat16"),
+    "d0": ("sbuf", [128, EC], "float16"),
+    "slot": ("sbuf", [128, EC], "bfloat16"),
+    "pcol": ("sbuf", [128, 1], "int32"),
+    "gi": ("sbuf", [128, 1], "int32"),
+    "gf": ("sbuf", [128, 1], "float32"),
+    "ucol": ("sbuf", [128, 72], "bfloat16"),
+    "uu": ("sbuf", [128, 72], "bfloat16"),
+    "ut": ("sbuf", [128, 72], "bfloat16"),
+    "uv": ("sbuf", [128, 72], "bfloat16"),
+    "en": ("sbuf", [128, 72], "bfloat16"),
+    "ep": ("sbuf", [128, 72], "bfloat16"),
+    "wl": ("sbuf", [128, (S - 1) * 64], "bfloat16"),
+    "cst": ("sbuf", [128, 64], "bfloat16"),
+    "sraw": ("sbuf", [128, 128], "bfloat16"),
+    "sel": ("sbuf", [128, 128], "float16"),
+    "rmp": ("sbuf", [128, 256], "bfloat16"),
+    "rp": ("sbuf", [128, 256], "bfloat16"),
+    "rn": ("sbuf", [128, 256], "bfloat16"),
+    "idf": ("sbuf", [128, 128], "float16"),
+    "zb": ("sbuf", [128, 17 * NCH, 8], "bfloat16"),
+    "z": ("sbuf", [128, 17 * NCH, 8], "float16"),
+    "back": ("sbuf", [128, 2 * CC], "bfloat16"),
+    "over": ("sbuf", [128, 256], "float32"),
+    "ypb": ("sbuf", [128, 256], "float32"),
+}
+for _c in range(NCH):
+    SCRATCH["pp%d" % _c] = ("psum", [128, 512], "float32")
+for _c in range(2):
+    SCRATCH["pc%d" % _c] = ("psum", [128, 512], "float32")
+    SCRATCH["po%d" % _c] = ("psum", [128, 512], "float32")
+
+SEMAPHORES = ["l_ring", "l_pa", "l_pb", "l_carry", "l_ext", "io_a", "io_b", "io_c", "vs", "wts", "pfa", "pfb",
+              "dei", "st"]
+for _c in range(NCH):
+    SEMAPHORES += ["%s%d" % (_k, _c) for _k in ("gs", "gv", "ins", "sc", "fp", "mc", "mf", "ev", "zo", "mp", "up")]
+for _t in range(1, RO):
+    SEMAPHORES += ["arr%d_%d" % (_t, _c) for _c in range(NCH)] + ["sent%d" % _t, "fix%d" % _t]
+
+
+def rank_program(g, core, T, topo):
+    rank = T.rank_of(core)
+    if rank is None:
+        return
+    N = len(T.cores)
+    V, A, PE, SY = g.vector, g.scalar, g.tensor, g.sync
+    sem = T.sem
+    seen = {}
+
+    def wait(q, qn, name, val):
+        if val > seen.get((qn, name), 0):
+            q.wait_ge(sem[name], val)
+            seen[(qn, name)] = val
+
+    def wait_item(q, qn, kind, i):
+        if i >= 0:
+            wait(q, qn, "%s%d" % (kind, i % NCH), i // NCH + 1)
+
+    def dest(r, t):
+        return T.cores[(r + 1 + t % (N - 1)) % N]
+
+    def common(c):
+        m = -1
+        for o in T.cores:
+            if o != c:
+                assert topo.may_write(c, o)
+                m &= topo.mask(c, o)
+        return m
+
+    def neng(c):
+        return bin(common(c)).count("1")
+
+    H = 2 * CC
+    A.dma_start(T.pl[:, 0:H], T.place[:, 0:H]).then_inc(sem.l_pa, 16)
+    SY.dma_start(T.win[:, 0:W], T.ring[:, :]).then_inc(sem.l_ring, 16)
+    SY.dma_start(T.land[:, 0:J], T.carry[:, :]).then_inc(sem.l_carry, 16)
+    SY.dma_start(T.pl[:, H:2 * H], T.place[:, H:2 * H]).then_inc(sem.l_pb, 16)
+    SY.dma_start(T.win[:, W:WX], T.ring[:, 0:WX - W]).then_inc(sem.l_ext, 16)
+
+    small = dict(allow_small_or_imprecise_dtypes=True)
+    g.iota(T.pcol[:], [[1, 1]], 0, 1).then_inc(sem.io_a, 1)
+    g.iota(T.ucol[:], [[1, 72]], 0, 0, **small).then_inc(sem.io_a, 1)
+    g.iota(T.rmp[:], [[0, 2], [1, 128]], 0, -1, **small).then_inc(sem.io_b, 1)
+    g.iota(T.sraw[:], [[1, 2], [2, 64]], 0, -1, **small).then_inc(sem.io_b, 1)
+    g.iota(T.slot[:], [[0, JC], [1, S]], 0, 0, **small).then_inc(sem.io_c, 1)
+
+    nv = [0]
+
+    def vs(ins):
+        ins.then_inc(sem.vs, 1)
+        nv[0] += 1
+
+    def vsync():
+        wait(V, "V", "vs", nv[0])
+
+    nw = [0]
+
+    def wts(ins):
+        ins.then_inc(sem.wts, 1)
+        nw[0] += 1
+
+    vs(V.memset(T.zb[:], 0.0))
+    wts(V.memset(T.back[:, 0:CC], MID - RO * DRIFT))
+    wts(V.memset(T.back[:, CC:2 * CC], MID))
+    for c in range(NCH):
+        if EXACT[c]:
+            V.memset(T.de[:, c * EC:(c + 1) * EC], -512.0).then_inc(sem.dei, 1)
+    wait(V, "V", "io_a", 2)
+    vs(V.tensor_scalar(T.gi[:], T.pcol[:], 0x70, 1, ALU.bitwise_and, ALU.logical_shift_right))
+    vsync()
+    vs(V.tensor_copy(T.gf[:], T.gi[:]))
+    vs(V.tensor_copy(T.z[:], T.zb[:]))
+    vsync()
+    vs(V.tensor_scalar(T.uu[:], T.ucol[:], T.gf[:], None, ALU.subtract))
+    vsync()
+    wts(V.tensor_scalar(T.en[:], T.uu[:], 7.0, -1.0, ALU.is_equal, ALU.mult))
+    wts(V.tensor_scalar(T.ep[:], T.uu[:], 7.0, None, ALU.is_equal))
+    vs(V.tensor_scalar(T.ut[:], T.uu[:], 7.0, -128.0, ALU.is_gt, ALU.mult))
+    wait(V, "V", "io_b", 2)
+    wts(V.tensor_scalar(T.rp[:], T.rmp[:], 0.0, None, ALU.is_equal))
+    wts(V.tensor_scalar(T.rn[:], T.rmp[:], 0.0, -1.0, ALU.is_equal, ALU.mult))
+    wts(V.tensor_scalar(T.idf[:], T.rmp[:, 0:128], 0.0, None, ALU.is_equal))
+    wts(V.tensor_scalar(T.sel[:], T.sraw[:], 0.0, None, ALU.is_equal))
+    vsync()
+    vs(V.tensor_tensor(T.uv[:], T.uu[:], T.ut[:], ALU.add))
+
+    def first_lists(half, ld, done):
+        wait(V, "V", ld, 16)
+        for c in (2 * half, 2 * half + 1):
+            V.tensor_copy(T.off[:, c * CC:(c + 1) * CC], T.pl[:, c * CC:(c + 1) * CC]).then_inc(sem["up%d" % c], 1)
+        V.tensor_scalar(T.plf[:, half * H:(half + 1) * H], T.pl[:, half * H:(half + 1) * H], -MID, None, ALU.add
+                        ).then_inc(sem[done], 1)
+
+    first_lists(0, "l_pa", "pfa")
+    vsync()
+    for m in range(S - 1):
+        wts(V.tensor_scalar(T.wl[:, m * 64:(m + 1) * 64], T.uv[:, 0:64], float(m + 1), None, ALU.is_ge))
+    wait(V, "V", "io_c", 1)
+    wts(V.tensor_scalar(T.cst[:], T.slot[:, 0:64], 1.0, 16 * M, ALU.is_ge, ALU.mult))
+    vs(V.tensor_scalar(T.d0[:], T.slot[:], 0.0, M - 8.0, ALU.is_equal, ALU.mult))
+
+    def ring_ready(q, qn, t):
+        wait(q, qn, "l_ring", 16)
+        if t > 0:
+            wait(q, qn, "l_ext", 16)
+
+    def carry_cols(i):
+        return slice(i * JC, (i + 1) * JC)
+
+    def slot_of(buf, c, m):
+        return buf[:, c * EC + m:(c + 1) * EC:S]
+
+    def gather_s(i):
+        t, c = divmod(i, NCH)
+        v = VSHARE[i]
+        ring_ready(A, "A", t)
+        wait_item(A, "A", "up", i)
+        A.activation(T.d1[:, c * EC + v:(c + 1) * EC],
+                     T.win[:, 0:W + MOVE * t].indirect(T.off[:, c * CC + v // 16:(c + 1) * CC]),
+                     ACT.Identity, bias=BIAS).then_inc(sem["gs%d" % c], 1)
+
+    def gather_v(i):
+        t, c = divmod(i, NCH)
+        v = VSHARE[i]
+        ring_ready(V, "V", t)
+        wait_item(V, "V", "up", i)
+        V.tensor_scalar(T.d1[:, c * EC:c * EC + v],
+                        T.win[:, 0:W + MOVE * t].indirect(T.off[:, c * CC:c * CC + v // 16]),
+                        BIAS, None, ALU.add).then_inc(sem["gv%d" % c], 1)
+
+    def arrived(q, qn, i):
+        t, c = divmod(i, NCH)
+        if t == 0:
+            wait(q, qn, "l_carry", 16)
+        else:
+            sender = T.cores[(rank - 1 - (t - 1) % (N - 1)) % N]
+            wait(q, qn, "arr%d_%d" % (t, c), neng(sender))
+
+    def add_carry(i):
+        c = i % NCH
+        if EXACT[c]:
+            return
+        arrived(V, "V", i)
+        vsync()
+        wait_item(V, "V", "gv", i)
+        wait_item(V, "V", "gs", i)
+        s0 = slot_of(T.d1, c, 0)
+        if ADD_BY_SCAN:
+            ins = V.tensor_tensor_scan(s0, T.land[:, carry_cols(i)], s0, 0.0, ALU.max, ALU.add)
+        else:
+            ins = V.tensor_tensor(s0, s0, T.land[:, carry_cols(i)], ALU.add)
+        ins.then_inc(sem["ins%d" % c], 1)
+
+    def put_carry(i):
+        c = i % NCH
+        if not EXACT[c]:
+            return
+        wait(g, "G", "dei", sum(EXACT))
+        wait_item(g, "G", "sc", i - NCH)
+        arrived(g, "G", i)
+        g.affine_select(slot_of(T.de, c, 0), T.land[:, carry_cols(i)], [[0, JC]], ALU.is_ge, 0.0, 0, 0
+                        ).then_inc(sem["ins%d" % c], 1)
+
+    def scan(i):
+        c = i % NCH
+        cols = slice(c * EC, (c + 1) * EC)
+        vsync()
+        for k in ("gv", "gs", "ins"):
+            wait_item(V, "V", k, i)
+        if EXACT[c]:
+            V.tensor_tensor_scan(T.vv[:, cols], T.de[:, cols], T.d1[:, cols], -512.0, ALU.max, ALU.add
+                                 ).then_inc(sem["sc%d" % c], 1)
+            wait_item(V, "V", "sc", i)
+            V.tensor_scalar(T.fo[:, cols], T.vv[:, cols], M - 7.5, None, ALU.add).then_inc(sem["fp%d" % c], 1)
+        else:
+            V.tensor_tensor_scan(T.fo[:, cols], T.d0[:], T.d1[:, cols], 0.0, ALU.max, ALU.add
+                                 ).then_inc(sem["sc%d" % c], 1)
+
+    def lists(i):
+        t, c = divmod(i, NCH)
+        cols = slice(c * CC, (c + 1) * CC)
+        bank = T["pp%d" % c][:, 0:CC]
+        wait_item(V, "V", "mp", i)
+        if t < RO - 1:
+            V.tensor_scalar(T.off[:, cols], bank, MID - (0.0 if EXACT[c] else DRIFT * (t + 1)), None, ALU.add
+                            ).then_inc(sem["up%d" % c], 1)
+        else:
+            vs(V.tensor_scalar(T.over[:, cols], bank, float(W), -float(W), ALU.is_ge, ALU.mult))
+            vsync()
+            V.tensor_tensor(T.ypb[:, cols], bank, T.over[:, cols], ALU.add).then_inc(sem["up%d" % c], 1)
+
+    halves = [c for c in range(NCH) if not EXACT[c]]
+
+    def unhalve(t):
+        if halves:
+            cols = slice(t * J + halves[0] * JC, t * J + (halves[-1] + 1) * JC)
+            for c in halves:
+                wait_item(V, "V", "ev", t * NCH + c)
+            V.tensor_scalar(T.outy[:, cols], T.outc[:, cols], -0.5, None, ALU.add).then_inc(sem["fix%d" % (t + 1)], 1)
+
+    def evacuate(i):
+        t, c = divmod(i, NCH)
+        wait_item(A, "A", "mc", i)
+        bias = M if EXACT[c] or t < RO - 1 else M - 0.5
+        A.activation(T.outc[:, carry_cols(i)], T["pc%d" % (i % 2)][:, 0:JC], ACT.Identity, bias=bias
+                     ).then_inc(sem["ev%d" % c], 1)
+
+    def moves(i):
+        c = i % NCH
+        z = T.z[:, 17 * c + 1:17 * c + 17:2, :]
+        wait_item(V, "V", "mf", i)
+        V.tensor_tensor(z, T["po%d" % (i % 2)][:, 0:64], z, ALU.add).then_inc(sem["zo%d" % c], 1)
+
+    def to_lists(i):
+        if i < 0:
+            return
+        t, c = divmod(i, NCH)
+        bank = T["pp%d" % c][:, 0:CC]
+        wait(PE, "P", "pfa" if c < 2 else "pfb", 1)
+        wait_item(PE, "P", "up", i)
+        PE.matmul(bank, T.idf[:], T.plf[:, c * CC:(c + 1) * CC], True, False)
+        if t == RO - 1:
+            b0 = CC if EXACT[c] else 0
+            PE.matmul(bank, T.rp[:, 0:128], T.back[:, b0:b0 + CC], False, False)
+        wait_item(PE, "P", "zo", i)
+        PE.matmul(bank, T.z[:, 17 * c + 1:17 * c + 17, :], T.sel[:, 0:64], False, False)
+        PE.matmul(bank, T.z[:, 17 * c:17 * c + 16, :], T.sel[:, 64:128], False, True).then_inc(sem["mp%d" % c], 1)
+
+    def matmuls(i):
+        t, c = divmod(i, NCH)
+        ob = T["po%d" % (i % 2)][:, 0:64]
+        cb = T["pc%d" % (i % 2)][:, 0:JC]
+        r0 = 112 if t < RO - 1 else 0
+        rot, nrot = T.rp[:, r0:r0 + 128], T.rn[:, r0:r0 + 128]
+        wait(PE, "P", "wts", nw[0])
+        wait_item(PE, "P", "zo", i - 2)
+        wait_item(PE, "P", "ev", i - 2)
+        PE.matmul(ob, T.rp[:, 0:128], T.cst[:], True, False)
+        if EXACT[c]:
+            wait_item(PE, "P", "ins", i)
+            PE.matmul(ob, T.land[:, carry_cols(i)], T.ep[:, 7:71], False, False)
+            to_lists(i - 1)
+            wait_item(PE, "P", "sc", i)
+            PE.matmul(cb, rot, slot_of(T.vv, c, S - 1), True, False)
+            for k in range(1, S):
+                PE.matmul(ob, slot_of(T.vv, c, k - 1), T.ep[:, 7 - k:71 - k], False, False)
+            wait_item(PE, "P", "fp", i)
+        else:
+            wait_item(PE, "P", "gv", i)
+            wait_item(PE, "P", "gs", i)
+            for m in range(1, S):
+                PE.matmul(cb, rot, slot_of(T.d1, c, m), m == 1, False)
+            for m in range(1, S - 1):
+                PE.matmul(ob, slot_of(T.d1, c, m), T.wl[:, m * 64:(m + 1) * 64], False, False)
+            to_lists(i - 1)
+            wait_item(PE, "P", "ins", i)
+            PE.matmul(cb, rot, slot_of(T.d1, c, 0), False, False)
+            PE.matmul(ob, slot_of(T.d1, c, 0), T.wl[:, 0:64], False, False)
+            PE.matmul(ob, T.land[:, carry_cols(i)], T.ep[:, 7:71], False, False)
+            wait_item(PE, "P", "sc", i)
+        PE.matmul(cb, nrot, slot_of(T.fo, c, S - 1), False, True).then_inc(sem["mc%d" % c], 1)
+        for k in range(1, S):
+            ins = PE.matmul(ob, slot_of(T.fo, c, k - 1), T.en[:, 7 - k:71 - k], False, k == S - 1)
+        ins.then_inc(sem["mf%d" % c], 1)
+
+    def send(i):
+        t, c = divmod(i, NCH)
+        rid, pid, _ = topo.addr(dest(rank, t))
+        wait_item(g, "G", "ev", i)
+        g.remote_dma(T.land[:, carry_cols(i + NCH)], T.outc[:, carry_cols(i)],
+                     sem["arr%d_%d" % (t + 1, c)], sem["sent%d" % (t + 1)], pid, rid, common(core))
+
+    gather_s(0)
+    for i in range(NI):
+        if i + 1 < NI:
+            gather_s(i + 1)
+        evacuate(i)
+
+    gather_v(0)
+    for i in range(NI):
+        if i == 0 and halves:
+            cols = slice(halves[0] * JC, (halves[-1] + 1) * JC)
+            wait(V, "V", "l_carry", 16)
+            vs(V.tensor_scalar(T.land[:, cols], T.land[:, cols], 0.5, None, ALU.add))
+        if i + 1 < NI:
+            gather_v(i + 1)
+        if i == 0:
+            first_lists(1, "l_pb", "pfb")
+        add_carry(i)
+        if i >= 1:
+            moves(i - 1)
+        if i >= 2:
+            lists(i - 2)
+        scan(i)
+        if i % NCH == 1 and NCH <= i:
+            unhalve(i // NCH - 1)
+    lists(NI - 2)
+    moves(NI - 1)
+    lists(NI - 1)
+
+    for i in range(NI):
+        matmuls(i)
+    to_lists(NI - 1)
+
+    put_carry(0)
+    for i in range(NI):
+        if i + 1 < NI:
+            put_carry(i + 1)
+        if i < NI - NCH:
+            send(i)
+
+    ns = [0]
+
+    def store(q, out, in_):
+        q.dma_start(out, in_).then_inc(sem.st, 16)
+        ns[0] += 16
+
+    runs = []
+    for c in range(NCH):
+        if runs and runs[-1][0] == EXACT[c]:
+            runs[-1][2] = c + 1
+        else:
+            runs.append([EXACT[c], c, c + 1])
+    for t in range(RO - 1):
+        wait(SY, "S", "sent%d" % (t + 1), NCH * neng(core))
+        for c in range(NCH):
+            wait_item(SY, "S", "ev", t * NCH + c)
+        if halves:
+            wait(SY, "S", "fix%d" % (t + 1), 1)
+        for ex, c0, c1 in runs:
+            cols = slice(t * J + c0 * JC, t * J + c1 * JC)
+            src = T.outc if ex else T.outy
+            store(SY, T.yc[0:112, cols], src[16:128, cols])
+            store(SY, T.yc[112:128, cols], src[0:16, cols])
+    a, b, e = (RO - 1) * J, RO * J - JC, RO * J
+    for c in range(NCH - 1):
+        wait(SY, "S", "ev%d" % c, RO)
+    store(SY, T.yc[:, a:b], T.outc[:, a:b])
+    for c in range(NCH - 1):
+        wait(SY, "S", "up%d" % c, RO + 1)
+    store(SY, T.yp[:, 0:256 - CC], T.ypb[:, 0:256 - CC])
+    wait(A, "A", "ev%d" % (NCH - 1), RO)
+    store(A, T.yc[:, b:e], T.outc[:, b:e])
+    wait(SY, "S", "up%d" % (NCH - 1), RO + 1)
+    store(SY, T.yp[:, 256 - CC:256], T.ypb[:, 256 - CC:256])
+    wait(SY, "S", "st", ns[0])

@@ -5,53 +5,54 @@ NCH = 4
 JC = J // NCH
 CC = JC * S // 16
 EC = JC * S
+ZB = 18
 MOVE = 240
 WX = W + MOVE * (RO - 1)
 NI = RO * NCH
 M = 3072.0
-BIAS = -32.0
+BIAS = -32.0 + 1.0 / 16
+LOW = -32768.0
+LIFT = M / 2
 MID = 2048.0
-DRIFT = 8.0
-VSHARE = [384, 320, 448, 352] + [352, 320, 320, 320] * 6 + [384, 352, 320, 256]
-EXACT = [False, False, False, False]
-ADD_BY_SCAN = True
+VSHARE = [544, 320, 448, 384, 416, 288] + [384] * 24 + [320, 544]
+VFIRST = [0] * 32
+EARLY = 2
+SSTART = 0
 
 SCRATCH = {
     "win": ("sbuf", [128, WX], "bfloat16"),
     "pl": ("sbuf", [128, 256], "int32"),
-    "plf": ("sbuf", [128, 256], "float16"),
+    "plx": ("sbuf", [128, J], "float16"),
     "off": ("sbuf", [128, 256], "uint16"),
     "land": ("sbuf", [128, RO * J], "bfloat16"),
     "outc": ("sbuf", [128, RO * J], "bfloat16"),
-    "outy": ("sbuf", [128, RO * J], "bfloat16"),
-    "d1": ("sbuf", [128, J * S], "bfloat16"),
+    "d1": ("sbuf", [128, J * S], "float16"),
     "fo": ("sbuf", [128, J * S], "bfloat16"),
-    "vv": ("sbuf", [128, J * S], "bfloat16"),
-    "de": ("sbuf", [128, J * S], "bfloat16"),
     "d0": ("sbuf", [128, EC], "float16"),
-    "slot": ("sbuf", [128, EC], "bfloat16"),
-    "pcol": ("sbuf", [128, 1], "int32"),
-    "gi": ("sbuf", [128, 1], "int32"),
-    "gf": ("sbuf", [128, 1], "float32"),
-    "ucol": ("sbuf", [128, 72], "bfloat16"),
-    "uu": ("sbuf", [128, 72], "bfloat16"),
-    "ut": ("sbuf", [128, 72], "bfloat16"),
-    "uv": ("sbuf", [128, 72], "bfloat16"),
-    "en": ("sbuf", [128, 72], "bfloat16"),
-    "ep": ("sbuf", [128, 72], "bfloat16"),
-    "wl": ("sbuf", [128, (S - 1) * 64], "bfloat16"),
-    "cst": ("sbuf", [128, 64], "bfloat16"),
-    "sraw": ("sbuf", [128, 128], "bfloat16"),
-    "sel": ("sbuf", [128, 128], "float16"),
-    "rmp": ("sbuf", [128, 256], "bfloat16"),
-    "rp": ("sbuf", [128, 256], "bfloat16"),
-    "rn": ("sbuf", [128, 256], "bfloat16"),
-    "idf": ("sbuf", [128, 128], "float16"),
-    "zb": ("sbuf", [128, 17 * NCH, 8], "bfloat16"),
-    "z": ("sbuf", [128, 17 * NCH, 8], "float16"),
-    "back": ("sbuf", [128, 2 * CC], "bfloat16"),
+    "z": ("sbuf", [128, ZB * (NCH + 1), 8], "float16"),
     "over": ("sbuf", [128, 256], "float32"),
     "ypb": ("sbuf", [128, 256], "float32"),
+    "pcol": ("sbuf", [128, 1], "int32"),
+    "gi": ("sbuf", [128, 5], "int32"),
+    "gf": ("sbuf", [128, 5], "float32"),
+    "cols": ("sbuf", [128, 2], "float32"),
+    "rmp": ("sbuf", [128, 256], "bfloat16"),
+    "sraw": ("sbuf", [128, 128], "bfloat16"),
+    "graw": ("sbuf", [128, 8, 8], "bfloat16"),
+    "ucol": ("sbuf", [128, 144], "bfloat16"),
+    "tcol": ("sbuf", [128, RO], "float32"),
+    "span": ("sbuf", [128, JC], "bfloat16"),
+    "rp": ("sbuf", [128, 128], "bfloat16"),
+    "rph": ("sbuf", [128, 256], "float16"),
+    "rn": ("sbuf", [128, 256], "bfloat16"),
+    "sel": ("sbuf", [128, 128], "float16"),
+    "en": ("sbuf", [128, 72], "bfloat16"),
+    "ep": ("sbuf", [128, 72], "bfloat16"),
+    "ed": ("sbuf", [128, 144], "bfloat16"),
+    "ey": ("sbuf", [128, 72], "float16"),
+    "wl": ("sbuf", [128, S - 1, 8, 8], "float16"),
+    "kc": ("sbuf", [128, RO], "float32"),
+    "back": ("sbuf", [128, 2, CC], "bfloat16"),
 }
 for _c in range(NCH):
     SCRATCH["pp%d" % _c] = ("psum", [128, 512], "float32")
@@ -59,12 +60,11 @@ for _c in range(2):
     SCRATCH["pc%d" % _c] = ("psum", [128, 512], "float32")
     SCRATCH["po%d" % _c] = ("psum", [128, 512], "float32")
 
-SEMAPHORES = ["l_ring", "l_pa", "l_pb", "l_carry", "l_ext", "io_a", "io_b", "io_c", "vs", "wts", "pfa", "pfb",
-              "dei", "st"]
+SEMAPHORES = ["l_ring", "l_pl", "l_carry", "l_ext", "io_a", "io_b", "io_c", "io_d", "vs", "wts", "plx", "plm", "plz",
+              "late", "st", "sent", "ov"]
 for _c in range(NCH):
-    SEMAPHORES += ["%s%d" % (_k, _c) for _k in ("gs", "gv", "ins", "sc", "fp", "mc", "mf", "ev", "zo", "mp", "up")]
-for _t in range(1, RO):
-    SEMAPHORES += ["arr%d_%d" % (_t, _c) for _c in range(NCH)] + ["sent%d" % _t, "fix%d" % _t]
+    SEMAPHORES += ["%s%d" % (_k, _c) for _k in ("ga", "ins", "sc", "mc", "mf", "ev", "zo", "mp", "up")]
+SEMAPHORES += ["arr%d" % _i for _i in range(NCH, NI)] + ["sent%d" % _t for _t in range(RO)]
 
 
 def rank_program(g, core, T, topo):
@@ -75,6 +75,7 @@ def rank_program(g, core, T, topo):
     V, A, PE, SY = g.vector, g.scalar, g.tensor, g.sync
     sem = T.sem
     seen = {}
+    last = NI - 1
 
     def wait(q, qn, name, val):
         if val > seen.get((qn, name), 0):
@@ -99,19 +100,18 @@ def rank_program(g, core, T, topo):
     def neng(c):
         return bin(common(c)).count("1")
 
-    H = 2 * CC
-    A.dma_start(T.pl[:, 0:H], T.place[:, 0:H]).then_inc(sem.l_pa, 16)
+    A.dma_start(T.pl[:], T.place[:, :]).then_inc(sem.l_pl, 16)
     SY.dma_start(T.win[:, 0:W], T.ring[:, :]).then_inc(sem.l_ring, 16)
     SY.dma_start(T.land[:, 0:J], T.carry[:, :]).then_inc(sem.l_carry, 16)
-    SY.dma_start(T.pl[:, H:2 * H], T.place[:, H:2 * H]).then_inc(sem.l_pb, 16)
     SY.dma_start(T.win[:, W:WX], T.ring[:, 0:WX - W]).then_inc(sem.l_ext, 16)
 
     small = dict(allow_small_or_imprecise_dtypes=True)
     g.iota(T.pcol[:], [[1, 1]], 0, 1).then_inc(sem.io_a, 1)
-    g.iota(T.ucol[:], [[1, 72]], 0, 0, **small).then_inc(sem.io_a, 1)
     g.iota(T.rmp[:], [[0, 2], [1, 128]], 0, -1, **small).then_inc(sem.io_b, 1)
-    g.iota(T.sraw[:], [[1, 2], [2, 64]], 0, -1, **small).then_inc(sem.io_b, 1)
-    g.iota(T.slot[:], [[0, JC], [1, S]], 0, 0, **small).then_inc(sem.io_c, 1)
+    g.iota(T.sraw[:], [[1, 2], [2, 64]], 0, -1, **small).then_inc(sem.io_c, 1)
+    g.iota(T.graw[:], [[8, 8], [0, 8]], 0, 0, **small).then_inc(sem.io_d, 1)
+    g.iota(T.ucol[:], [[1, 144]], -16, 0, **small).then_inc(sem.io_d, 1)
+    g.iota(T.tcol[:], [[-1, RO]], -1, 0, **small).then_inc(sem.io_d, 1)
 
     nv = [0]
 
@@ -128,45 +128,53 @@ def rank_program(g, core, T, topo):
         ins.then_inc(sem.wts, 1)
         nw[0] += 1
 
-    vs(V.memset(T.zb[:], 0.0))
-    wts(V.memset(T.back[:, 0:CC], MID - RO * DRIFT))
-    wts(V.memset(T.back[:, CC:2 * CC], MID))
-    for c in range(NCH):
-        if EXACT[c]:
-            V.memset(T.de[:, c * EC:(c + 1) * EC], -512.0).then_inc(sem.dei, 1)
-    wait(V, "V", "io_a", 2)
-    vs(V.tensor_scalar(T.gi[:], T.pcol[:], 0x70, 1, ALU.bitwise_and, ALU.logical_shift_right))
+    def lcols(c):
+        return slice(c * CC, (c + 1) * CC)
+
+    vs(V.memset(T.d0[:], LOW))
+    vs(V.memset(T.wl[:], 0.0))
+    vs(V.memset(T.span[:], -2 * M))
+    wait(V, "V", "io_a", 1)
+    G8, STAGE, ODD, G16, UPPER = (slice(k, k + 1) for k in range(5))
+    vs(V.tensor_scalar(T.gi[:, G8], T.pcol[:], 0x70, 1, ALU.bitwise_and, ALU.logical_shift_right))
+    vs(V.tensor_scalar(T.gi[:, STAGE], T.pcol[:], S - 1, None, ALU.bitwise_and))
+    vs(V.tensor_scalar(T.gi[:, ODD], T.pcol[:], 1, None, ALU.bitwise_and))
+    vs(V.tensor_scalar(T.gi[:, G16], T.pcol[:], 0x70, None, ALU.bitwise_and))
+    vs(V.tensor_scalar(T.gi[:, UPPER], T.pcol[:], 3, 1, ALU.logical_shift_right, ALU.bitwise_and))
+    wait(V, "V", "io_b", 1)
+    wts(V.tensor_scalar(T.rph[:], T.rmp[:], 0.0, None, ALU.is_equal))
+    wts(V.tensor_scalar(T.rn[:], T.rmp[:], 0.0, -1.0, ALU.is_equal, ALU.mult))
     vsync()
     vs(V.tensor_copy(T.gf[:], T.gi[:]))
-    vs(V.tensor_copy(T.z[:], T.zb[:]))
-    vsync()
-    vs(V.tensor_scalar(T.uu[:], T.ucol[:], T.gf[:], None, ALU.subtract))
-    vsync()
-    wts(V.tensor_scalar(T.en[:], T.uu[:], 7.0, -1.0, ALU.is_equal, ALU.mult))
-    wts(V.tensor_scalar(T.ep[:], T.uu[:], 7.0, None, ALU.is_equal))
-    vs(V.tensor_scalar(T.ut[:], T.uu[:], 7.0, -128.0, ALU.is_gt, ALU.mult))
-    wait(V, "V", "io_b", 2)
-    wts(V.tensor_scalar(T.rp[:], T.rmp[:], 0.0, None, ALU.is_equal))
-    wts(V.tensor_scalar(T.rn[:], T.rmp[:], 0.0, -1.0, ALU.is_equal, ALU.mult))
-    wts(V.tensor_scalar(T.idf[:], T.rmp[:, 0:128], 0.0, None, ALU.is_equal))
+    wts(V.tensor_scalar(T.rp[:], T.rmp[:, 0:128], 0.0, None, ALU.is_equal))
+    wait(V, "V", "io_c", 1)
     wts(V.tensor_scalar(T.sel[:], T.sraw[:], 0.0, None, ALU.is_equal))
     vsync()
-    vs(V.tensor_tensor(T.uv[:], T.uu[:], T.ut[:], ALU.add))
-
-    def first_lists(half, ld, done):
-        wait(V, "V", ld, 16)
-        for c in (2 * half, 2 * half + 1):
-            V.tensor_copy(T.off[:, c * CC:(c + 1) * CC], T.pl[:, c * CC:(c + 1) * CC]).then_inc(sem["up%d" % c], 1)
-        V.tensor_scalar(T.plf[:, half * H:(half + 1) * H], T.pl[:, half * H:(half + 1) * H], -MID, None, ALU.add
-                        ).then_inc(sem[done], 1)
-
-    first_lists(0, "l_pa", "pfa")
+    vs(V.tensor_scalar(T.d0[:, 0:EC:S], T.span[:], T.gf[:, ODD], M - 8.0, ALU.mult, ALU.add))
+    vs(V.tensor_scalar(T.cols[:, 0:1], T.gf[:, ODD], -2 * M, M - 0.5, ALU.mult, ALU.add))
+    vs(V.tensor_scalar(T.cols[:, 1:2], T.gf[:, UPPER], -1.0, 1.0, ALU.mult, ALU.add))
+    V.tensor_scalar(T.ey[:], T.rmp[:, 0:72], T.gf[:, G8], 0.0, ALU.add, ALU.is_equal).then_inc(sem.plx, 1)
+    wait(V, "V", "l_pl", 16)
+    V.tensor_scalar(T.plx[:, 0:J:2], T.pl[:], -MID, T.gf[:, UPPER], ALU.add, ALU.mult).then_inc(sem.plx, 1)
     vsync()
+    V.tensor_scalar(T.plx[:, 1:J:2], T.pl[:], -MID, T.cols[:, 1:2], ALU.add, ALU.mult).then_inc(sem.plx, 1)
+    for c in range(NCH):
+        V.tensor_copy(T.off[:, lcols(c)], T.pl[:, lcols(c)]).then_inc(sem["up%d" % c], 1)
+    wait(V, "V", "io_d", 3)
+    vs(V.tensor_scalar(T.kc[:], T.tcol[:], T.gf[:, STAGE], MID, ALU.mult, ALU.add))
     for m in range(S - 1):
-        wts(V.tensor_scalar(T.wl[:, m * 64:(m + 1) * 64], T.uv[:, 0:64], float(m + 1), None, ALU.is_ge))
-    wait(V, "V", "io_c", 1)
-    wts(V.tensor_scalar(T.cst[:], T.slot[:, 0:64], 1.0, 16 * M, ALU.is_ge, ALU.mult))
-    vs(V.tensor_scalar(T.d0[:], T.slot[:], 0.0, M - 8.0, ALU.is_equal, ALU.mult))
+        wts(V.tensor_scalar(T.wl[:, m, :, m + 1:S], T.graw[:, :, m + 1:S], T.gf[:, G8], None, ALU.is_equal))
+    wts(V.tensor_scalar(T.en[:], T.ucol[:, 9:81], T.gf[:, G8], -1.0, ALU.is_equal, ALU.mult))
+    wts(V.tensor_scalar(T.ep[:], T.ucol[:, 9:81], T.gf[:, G8], None, ALU.is_equal))
+    vsync()
+    ready = nv[0]
+
+    def late_constants():
+        V.tensor_scalar(T.ed[:], T.ucol[:], T.gf[:, G16], -1.0, ALU.is_equal, ALU.mult).then_inc(sem.late, 1)
+        V.memset(T.z[:, ZB * NCH:ZB * (NCH + 1), :], 0.0).then_inc(sem.late, 1)
+        for h in range(2):
+            V.tensor_scalar(T.back[:, h, :], T.span[:, 0:CC], h * LIFT / (2 * M), T.kc[:, RO - 1:RO],
+                            ALU.mult, ALU.add).then_inc(sem.late, 1)
 
     def ring_ready(q, qn, t):
         wait(q, qn, "l_ring", 16)
@@ -179,204 +187,214 @@ def rank_program(g, core, T, topo):
     def slot_of(buf, c, m):
         return buf[:, c * EC + m:(c + 1) * EC:S]
 
-    def gather_s(i):
-        t, c = divmod(i, NCH)
-        v = VSHARE[i]
-        ring_ready(A, "A", t)
-        wait_item(A, "A", "up", i)
-        A.activation(T.d1[:, c * EC + v:(c + 1) * EC],
-                     T.win[:, 0:W + MOVE * t].indirect(T.off[:, c * CC + v // 16:(c + 1) * CC]),
-                     ACT.Identity, bias=BIAS).then_inc(sem["gs%d" % c], 1)
+    def places(c):
+        return T["pp%d" % c][:, 0:CC]
 
-    def gather_v(i):
-        t, c = divmod(i, NCH)
-        v = VSHARE[i]
-        ring_ready(V, "V", t)
-        wait_item(V, "V", "up", i)
-        V.tensor_scalar(T.d1[:, c * EC:c * EC + v],
-                        T.win[:, 0:W + MOVE * t].indirect(T.off[:, c * CC:c * CC + v // 16]),
-                        BIAS, None, ALU.add).then_inc(sem["gv%d" % c], 1)
+    def sums(i):
+        return T["po%d" % (i % 2)][:, 0:64]
 
-    def arrived(q, qn, i):
+    def ends(i):
+        return T["pc%d" % (i % 2)][:, 0:JC]
+
+    def moved(b):
+        return T.z[:, ZB * b + 1:ZB * b + 17:2, :]
+
+    def gather(q, qn, i, a, b):
         t, c = divmod(i, NCH)
-        if t == 0:
-            wait(q, qn, "l_carry", 16)
+        ring_ready(q, qn, t)
+        wait_item(q, qn, "up", i)
+        src = T.win[:, 0:W + MOVE * t].indirect(T.off[:, c * CC + a // 16:c * CC + b // 16])
+        out = T.d1[:, c * EC + a:c * EC + b]
+        if q is V:
+            ins = V.tensor_scalar(out, src, BIAS, None, ALU.add)
         else:
-            sender = T.cores[(rank - 1 - (t - 1) % (N - 1)) % N]
-            wait(q, qn, "arr%d_%d" % (t, c), neng(sender))
+            ins = A.activation(out, src, ACT.Identity, bias=BIAS)
+        ins.then_inc(sem["ga%d" % c], 1)
+
+    def gather_s(i):
+        gather(A, "A", i, VSHARE[i], EC)
+
+    def gather_v(i, a, b):
+        if a < b:
+            gather(V, "V", i, a, b)
+
+    def gathered(q, qn, i):
+        calls = [1 + (k == 0) + (k > 0) * ((0 < min(VSHARE[k], VFIRST[k - 1])) + (VFIRST[k - 1] < VSHARE[k]))
+                 for k in range(i % NCH, i + 1, NCH)]
+        wait(q, qn, "ga%d" % (i % NCH), sum(calls))
 
     def add_carry(i):
-        c = i % NCH
-        if EXACT[c]:
-            return
-        arrived(V, "V", i)
-        vsync()
-        wait_item(V, "V", "gv", i)
-        wait_item(V, "V", "gs", i)
-        s0 = slot_of(T.d1, c, 0)
-        if ADD_BY_SCAN:
-            ins = V.tensor_tensor_scan(s0, T.land[:, carry_cols(i)], s0, 0.0, ALU.max, ALU.add)
+        t, c = divmod(i, NCH)
+        gathered(V, "V", i)
+        if t == 0:
+            wait(V, "V", "l_carry", 16)
         else:
-            ins = V.tensor_tensor(s0, s0, T.land[:, carry_cols(i)], ALU.add)
-        ins.then_inc(sem["ins%d" % c], 1)
-
-    def put_carry(i):
-        c = i % NCH
-        if not EXACT[c]:
-            return
-        wait(g, "G", "dei", sum(EXACT))
-        wait_item(g, "G", "sc", i - NCH)
-        arrived(g, "G", i)
-        g.affine_select(slot_of(T.de, c, 0), T.land[:, carry_cols(i)], [[0, JC]], ALU.is_ge, 0.0, 0, 0
-                        ).then_inc(sem["ins%d" % c], 1)
+            sender = T.cores[(rank - 1 - (t - 1) % (N - 1)) % N]
+            wait(V, "V", "arr%d" % i, neng(sender))
+        s0 = slot_of(T.d1, c, 0)
+        V.tensor_tensor_scan(s0, T.land[:, carry_cols(i)], s0, 0.0, ALU.max, ALU.add).then_inc(sem["ins%d" % c], 1)
 
     def scan(i):
         c = i % NCH
         cols = slice(c * EC, (c + 1) * EC)
-        vsync()
-        for k in ("gv", "gs", "ins"):
-            wait_item(V, "V", k, i)
-        if EXACT[c]:
-            V.tensor_tensor_scan(T.vv[:, cols], T.de[:, cols], T.d1[:, cols], -512.0, ALU.max, ALU.add
-                                 ).then_inc(sem["sc%d" % c], 1)
-            wait_item(V, "V", "sc", i)
-            V.tensor_scalar(T.fo[:, cols], T.vv[:, cols], M - 7.5, None, ALU.add).then_inc(sem["fp%d" % c], 1)
-        else:
-            V.tensor_tensor_scan(T.fo[:, cols], T.d0[:], T.d1[:, cols], 0.0, ALU.max, ALU.add
-                                 ).then_inc(sem["sc%d" % c], 1)
+        wait_item(V, "V", "ins", i)
+        V.tensor_tensor_scan(T.fo[:, cols], T.d0[:], T.d1[:, cols], LOW, ALU.max, ALU.add
+                             ).then_inc(sem["sc%d" % c], 1)
 
     def lists(i):
         t, c = divmod(i, NCH)
-        cols = slice(c * CC, (c + 1) * CC)
-        bank = T["pp%d" % c][:, 0:CC]
         wait_item(V, "V", "mp", i)
         if t < RO - 1:
-            V.tensor_scalar(T.off[:, cols], bank, MID - (0.0 if EXACT[c] else DRIFT * (t + 1)), None, ALU.add
+            V.tensor_scalar(T.off[:, lcols(c)], places(c), T.kc[:, t:t + 1], None, ALU.add
                             ).then_inc(sem["up%d" % c], 1)
         else:
-            vs(V.tensor_scalar(T.over[:, cols], bank, float(W), -float(W), ALU.is_ge, ALU.mult))
-            vsync()
-            V.tensor_tensor(T.ypb[:, cols], bank, T.over[:, cols], ALU.add).then_inc(sem["up%d" % c], 1)
+            V.tensor_scalar(T.over[:, lcols(c)], places(c), float(W), -float(W), ALU.is_ge, ALU.mult
+                            ).then_inc(sem.ov, 1)
 
-    halves = [c for c in range(NCH) if not EXACT[c]]
-
-    def unhalve(t):
-        if halves:
-            cols = slice(t * J + halves[0] * JC, t * J + (halves[-1] + 1) * JC)
-            for c in halves:
-                wait_item(V, "V", "ev", t * NCH + c)
-            V.tensor_scalar(T.outy[:, cols], T.outc[:, cols], -0.5, None, ALU.add).then_inc(sem["fix%d" % (t + 1)], 1)
+    def wrap(i):
+        c = i % NCH
+        wait(V, "V", "ov", c + 1)
+        V.tensor_tensor(T.ypb[:, lcols(c)], places(c), T.over[:, lcols(c)], ALU.add).then_inc(sem["up%d" % c], 1)
 
     def evacuate(i):
-        t, c = divmod(i, NCH)
         wait_item(A, "A", "mc", i)
-        bias = M if EXACT[c] or t < RO - 1 else M - 0.5
-        A.activation(T.outc[:, carry_cols(i)], T["pc%d" % (i % 2)][:, 0:JC], ACT.Identity, bias=bias
-                     ).then_inc(sem["ev%d" % c], 1)
+        A.activation(T.outc[:, carry_cols(i)], ends(i), ACT.Identity, bias=T.cols[:, 0:1]
+                     ).then_inc(sem["ev%d" % (i % NCH)], 1)
 
     def moves(i):
         c = i % NCH
-        z = T.z[:, 17 * c + 1:17 * c + 17:2, :]
-        wait_item(V, "V", "mf", i)
-        V.tensor_tensor(z, T["po%d" % (i % 2)][:, 0:64], z, ALU.add).then_inc(sem["zo%d" % c], 1)
-
-    def to_lists(i):
-        if i < 0:
-            return
-        t, c = divmod(i, NCH)
-        bank = T["pp%d" % c][:, 0:CC]
-        wait(PE, "P", "pfa" if c < 2 else "pfb", 1)
-        wait_item(PE, "P", "up", i)
-        PE.matmul(bank, T.idf[:], T.plf[:, c * CC:(c + 1) * CC], True, False)
-        if t == RO - 1:
-            b0 = CC if EXACT[c] else 0
-            PE.matmul(bank, T.rp[:, 0:128], T.back[:, b0:b0 + CC], False, False)
-        wait_item(PE, "P", "zo", i)
-        PE.matmul(bank, T.z[:, 17 * c + 1:17 * c + 17, :], T.sel[:, 0:64], False, False)
-        PE.matmul(bank, T.z[:, 17 * c:17 * c + 16, :], T.sel[:, 64:128], False, True).then_inc(sem["mp%d" % c], 1)
-
-    def matmuls(i):
-        t, c = divmod(i, NCH)
-        ob = T["po%d" % (i % 2)][:, 0:64]
-        cb = T["pc%d" % (i % 2)][:, 0:JC]
-        r0 = 112 if t < RO - 1 else 0
-        rot, nrot = T.rp[:, r0:r0 + 128], T.rn[:, r0:r0 + 128]
-        wait(PE, "P", "wts", nw[0])
-        wait_item(PE, "P", "zo", i - 2)
-        wait_item(PE, "P", "ev", i - 2)
-        PE.matmul(ob, T.rp[:, 0:128], T.cst[:], True, False)
-        if EXACT[c]:
-            wait_item(PE, "P", "ins", i)
-            PE.matmul(ob, T.land[:, carry_cols(i)], T.ep[:, 7:71], False, False)
-            to_lists(i - 1)
-            wait_item(PE, "P", "sc", i)
-            PE.matmul(cb, rot, slot_of(T.vv, c, S - 1), True, False)
-            for k in range(1, S):
-                PE.matmul(ob, slot_of(T.vv, c, k - 1), T.ep[:, 7 - k:71 - k], False, False)
-            wait_item(PE, "P", "fp", i)
+        wait_item(A, "A", "mf", i)
+        if i < last:
+            ins = A.activation(moved(c), sums(i), ACT.Identity)
         else:
-            wait_item(PE, "P", "gv", i)
-            wait_item(PE, "P", "gs", i)
-            for m in range(1, S):
-                PE.matmul(cb, rot, slot_of(T.d1, c, m), m == 1, False)
-            for m in range(1, S - 1):
-                PE.matmul(ob, slot_of(T.d1, c, m), T.wl[:, m * 64:(m + 1) * 64], False, False)
-            to_lists(i - 1)
-            wait_item(PE, "P", "ins", i)
-            PE.matmul(cb, rot, slot_of(T.d1, c, 0), False, False)
-            PE.matmul(ob, slot_of(T.d1, c, 0), T.wl[:, 0:64], False, False)
-            PE.matmul(ob, T.land[:, carry_cols(i)], T.ep[:, 7:71], False, False)
-            wait_item(PE, "P", "sc", i)
-        PE.matmul(cb, nrot, slot_of(T.fo, c, S - 1), False, True).then_inc(sem["mc%d" % c], 1)
+            ins = A.activation(moved(NCH), sums(i), ACT.Identity, bias=LIFT)
+        ins.then_inc(sem["zo%d" % c], 1)
+
+    def turn(buf, i):
+        r0 = 112 if i < NI - NCH else 0
+        return buf[:, r0:r0 + 128]
+
+    def mm_slots(i):
+        t, c = divmod(i, NCH)
+        wait_item(PE, "P", "ev", i - 2)
+        wait_item(PE, "P", "zo", i - 2)
+        gathered(PE, "P", i)
+        for m in range(1, S):
+            PE.matmul(ends(i), turn(T.rph, i), slot_of(T.d1, c, m), m == 1, False)
+        for m in range(1, S - 1):
+            PE.matmul(sums(i), slot_of(T.d1, c, m), T.wl[:, m], m == 1, False)
+        if t > 0 and i < last:
+            PE.matmul(sums(i), T.rph[:, 0:128], moved(c), False, False)
+
+    def mm_carry(i, close=False):
+        c = i % NCH
+        wait_item(PE, "P", "ins", i)
+        PE.matmul(sums(i), slot_of(T.d1, c, 0), T.wl[:, 0], False, False)
+        ins = PE.matmul(sums(i), T.land[:, carry_cols(i)], T.ep[:, 7:71], False, close)
+        if close:
+            ins.then_inc(sem["mf%d" % c], 1)
+        PE.matmul(ends(i), turn(T.rph, i), slot_of(T.d1, c, 0), False, False)
+
+    def mm_end(i):
+        c = i % NCH
+        wait_item(PE, "P", "sc", i)
+        PE.matmul(ends(i), turn(T.rn, i), slot_of(T.fo, c, S - 1), False, True).then_inc(sem["mc%d" % c], 1)
+
+    def mm_floors(i):
+        c = i % NCH
         for k in range(1, S):
-            ins = PE.matmul(ob, slot_of(T.fo, c, k - 1), T.en[:, 7 - k:71 - k], False, k == S - 1)
+            ins = PE.matmul(sums(i), slot_of(T.fo, c, k - 1), T.en[:, 7 - k:71 - k], False, k == S - 1)
         ins.then_inc(sem["mf%d" % c], 1)
 
-    def send(i):
+    def mm_floors_direct(i):
+        c = i % NCH
+        for s in range(2 * S):
+            if s % S:
+                PE.matmul(places(c), T.ed[:, 16 - s:144 - s], T.fo[:, c * EC + s - 1:(c + 1) * EC:2 * S], False, False)
+
+    def mm_select(c, b, start, stop):
+        PE.matmul(places(c), T.z[:, ZB * b + 1:ZB * b + 17, :], T.sel[:, 0:64], start, False)
+        return PE.matmul(places(c), T.z[:, ZB * b:ZB * b + 16, :], T.sel[:, 64:128], False, stop)
+
+    def mm_back(i):
+        c = i % NCH
+        wait(PE, "P", "late", 4)
+        wait_item(PE, "P", "up", i)
+        PE.matmul(places(c), T.rp[:], T.back[:, i // last, :], True, False)
+
+    def mm_places(i):
         t, c = divmod(i, NCH)
+        wait(PE, "P", "plz", 1)
+        wait_item(PE, "P", "up", i)
+        wait_item(PE, "P", "zo", i)
+        mm_select(c, c if i < last else NCH, t < RO - 1, True).then_inc(sem["mp%d" % c], 1)
+
+    def send(i):
+        t = i // NCH
         rid, pid, _ = topo.addr(dest(rank, t))
         wait_item(g, "G", "ev", i)
-        g.remote_dma(T.land[:, carry_cols(i + NCH)], T.outc[:, carry_cols(i)],
-                     sem["arr%d_%d" % (t + 1, c)], sem["sent%d" % (t + 1)], pid, rid, common(core))
+        g.remote_dma(T.land[:, carry_cols(i + NCH)], T.outc[:, carry_cols(i)], sem["arr%d" % (i + NCH)],
+                     sem["sent%d" % t if t < EARLY else "sent"], pid, rid, common(core))
 
+    first = T.pp0[:, 0:72 * NCH]
+    wait(A, "A", "plm", 1)
+    A.activation(T.z[:, 0:ZB * NCH:2, :], first, ACT.Identity).then_inc(sem.plz, 1)
     gather_s(0)
-    for i in range(NI):
-        if i + 1 < NI:
-            gather_s(i + 1)
+    gather_s(1)
+    wait(A, "A", "vs", ready)
+    for i in range(last):
+        if i + 2 < NI:
+            gather_s(i + 2)
         evacuate(i)
+        moves(i)
+    wait(A, "A", "late", 4)
+    moves(last)
+    evacuate(last)
 
-    gather_v(0)
+    gather_v(0, 0, VSHARE[0])
+    late_constants()
     for i in range(NI):
-        if i == 0 and halves:
-            cols = slice(halves[0] * JC, (halves[-1] + 1) * JC)
-            wait(V, "V", "l_carry", 16)
-            vs(V.tensor_scalar(T.land[:, cols], T.land[:, cols], 0.5, None, ALU.add))
-        if i + 1 < NI:
-            gather_v(i + 1)
-        if i == 0:
-            first_lists(1, "l_pb", "pfb")
+        v = VSHARE[i + 1] if i < last else 0
+        cut = min(v, VFIRST[i])
+        gather_v(i + 1, 0, cut)
         add_carry(i)
-        if i >= 1:
-            moves(i - 1)
+        gather_v(i + 1, cut, v)
         if i >= 2:
             lists(i - 2)
         scan(i)
-        if i % NCH == 1 and NCH <= i:
-            unhalve(i // NCH - 1)
-    lists(NI - 2)
-    moves(NI - 1)
-    lists(NI - 1)
+        if i - 2 >= NI - NCH:
+            wrap(i - 2)
+    for i in (last - 1, last):
+        lists(i)
+        wrap(i)
 
-    for i in range(NI):
-        matmuls(i)
-    to_lists(NI - 1)
+    wait(PE, "P", "plx", 3)
+    for c in range(NCH):
+        ins = PE.matmul(T.pp0[:, 72 * c:72 * (c + 1)], T.plx[:, c * JC:(c + 1) * JC], T.ey[:], True, True)
+    ins.then_inc(sem.plm, 1)
+    wait(PE, "P", "wts", nw[0])
+    for i in range(last):
+        mm_slots(i)
+        mm_carry(i)
+        if i - 1 >= NI - NCH:
+            mm_back(i - 1)
+        if i > 0:
+            mm_places(i - 1)
+        if i == last - 1:
+            mm_slots(last)
+        mm_end(i)
+        mm_floors(i)
+    mm_carry(last, close=True)
+    mm_back(last - 1)
+    mm_back(last)
+    mm_select(NCH - 1, NCH - 1, False, False)
+    mm_end(last)
+    mm_places(last - 1)
+    mm_floors_direct(last)
+    mm_places(last)
 
-    put_carry(0)
-    for i in range(NI):
-        if i + 1 < NI:
-            put_carry(i + 1)
-        if i < NI - NCH:
-            send(i)
+    for i in range(NI - NCH):
+        send(i)
 
     ns = [0]
 
@@ -384,23 +402,15 @@ def rank_program(g, core, T, topo):
         q.dma_start(out, in_).then_inc(sem.st, 16)
         ns[0] += 16
 
-    runs = []
-    for c in range(NCH):
-        if runs and runs[-1][0] == EXACT[c]:
-            runs[-1][2] = c + 1
-        else:
-            runs.append([EXACT[c], c, c + 1])
-    for t in range(RO - 1):
-        wait(SY, "S", "sent%d" % (t + 1), NCH * neng(core))
-        for c in range(NCH):
-            wait_item(SY, "S", "ev", t * NCH + c)
-        if halves:
-            wait(SY, "S", "fix%d" % (t + 1), 1)
-        for ex, c0, c1 in runs:
-            cols = slice(t * J + c0 * JC, t * J + c1 * JC)
-            src = T.outc if ex else T.outy
-            store(SY, T.yc[0:112, cols], src[16:128, cols])
-            store(SY, T.yc[112:128, cols], src[0:16, cols])
+    def store_back(cols):
+        store(SY, T.yc[0:112, cols], T.outc[16:128, cols])
+        store(SY, T.yc[112:128, cols], T.outc[0:16, cols])
+
+    for t in range(EARLY):
+        wait(SY, "S", "sent%d" % t, NCH * neng(core))
+        store_back(slice(t * J, (t + 1) * J))
+    wait(SY, "S", "sent", (RO - 1 - EARLY) * NCH * neng(core))
+    store_back(slice(EARLY * J, (RO - 1) * J))
     a, b, e = (RO - 1) * J, RO * J - JC, RO * J
     for c in range(NCH - 1):
         wait(SY, "S", "ev%d" % c, RO)

@@ -14,10 +14,13 @@ BIAS = -32.0 + 1.0 / 16
 LOW = -32768.0
 LIFT = M / 2
 MID = 2048.0
-VSHARE = [544, 320, 448, 384, 416, 288] + [384] * 24 + [320, 544]
-VFIRST = [0] * 32
+VSHARE = [576, 320, 416, 384] + [384, 384, 384, 352] * 6 + [352, 384, 352, 480]
+VFIRST = [160] + [0] * 31
 EARLY = 2
-SSTART = 0
+OPT = ["em", "escp", "ef"]
+TAIL = ["s", "", "01pz", "a29 g30 l27 s29 a30 g31 l28 d31 a31 s30 s31 x31 w28 l29 y31 w29 l30 l31 z31 w30 w31"]
+STAIL = "g30 e28 m28 g31 e29 m29 e30 m30 m31"
+OWN = [NI - 1]
 
 SCRATCH = {
     "win": ("sbuf", [128, WX], "bfloat16"),
@@ -29,20 +32,22 @@ SCRATCH = {
     "d1": ("sbuf", [128, J * S], "float16"),
     "fo": ("sbuf", [128, J * S], "bfloat16"),
     "d0": ("sbuf", [128, EC], "float16"),
+    "dz": ("sbuf", [128, EC], "bfloat16"),
+    "ve": ("sbuf", [128, J * S], "float16"),
+    "vq": ("sbuf", [128, J], "float16"),
     "z": ("sbuf", [128, ZB * (NCH + 1), 8], "float16"),
     "over": ("sbuf", [128, 256], "float32"),
     "ypb": ("sbuf", [128, 256], "float32"),
     "pcol": ("sbuf", [128, 1], "int32"),
     "gi": ("sbuf", [128, 5], "int32"),
     "gf": ("sbuf", [128, 5], "float32"),
-    "cols": ("sbuf", [128, 2], "float32"),
+    "cols": ("sbuf", [128, 4], "float32"),
     "rmp": ("sbuf", [128, 256], "bfloat16"),
     "sraw": ("sbuf", [128, 128], "bfloat16"),
     "graw": ("sbuf", [128, 8, 8], "bfloat16"),
     "ucol": ("sbuf", [128, 144], "bfloat16"),
     "tcol": ("sbuf", [128, RO], "float32"),
-    "span": ("sbuf", [128, JC], "bfloat16"),
-    "rp": ("sbuf", [128, 128], "bfloat16"),
+    "even": ("sbuf", [128, 1], "float32"),
     "rph": ("sbuf", [128, 256], "float16"),
     "rn": ("sbuf", [128, 256], "bfloat16"),
     "sel": ("sbuf", [128, 128], "float16"),
@@ -52,7 +57,7 @@ SCRATCH = {
     "ey": ("sbuf", [128, 72], "float16"),
     "wl": ("sbuf", [128, S - 1, 8, 8], "float16"),
     "kc": ("sbuf", [128, RO], "float32"),
-    "back": ("sbuf", [128, 2, CC], "bfloat16"),
+    "back": ("sbuf", [128, 2, CC], "float16"),
 }
 for _c in range(NCH):
     SCRATCH["pp%d" % _c] = ("psum", [128, 512], "float32")
@@ -61,9 +66,9 @@ for _c in range(2):
     SCRATCH["po%d" % _c] = ("psum", [128, 512], "float32")
 
 SEMAPHORES = ["l_ring", "l_pl", "l_carry", "l_ext", "io_a", "io_b", "io_c", "io_d", "vs", "wts", "plx", "plm", "plz",
-              "late", "st", "sent", "ov"]
+              "sa", "sb", "ed", "st", "sent", "dz", "own"]
 for _c in range(NCH):
-    SEMAPHORES += ["%s%d" % (_k, _c) for _k in ("ga", "ins", "sc", "mc", "mf", "ev", "zo", "mp", "up")]
+    SEMAPHORES += ["%s%d" % (_k, _c) for _k in ("ga", "ins", "sc", "mc", "mf", "ev", "zo", "mp", "up", "ov", "own")]
 SEMAPHORES += ["arr%d" % _i for _i in range(NCH, NI)] + ["sent%d" % _t for _t in range(RO)]
 
 
@@ -97,21 +102,25 @@ def rank_program(g, core, T, topo):
                 m &= topo.mask(c, o)
         return m
 
-    def neng(c):
-        return bin(common(c)).count("1")
+    def engines(c, i):
+        e = [k for k in range(common(c).bit_length()) if common(c) >> k & 1]
+        return sum(1 << k for k in e)
 
-    A.dma_start(T.pl[:], T.place[:, :]).then_inc(sem.l_pl, 16)
+    def neng(c, items):
+        return sum(bin(engines(c, i)).count("1") for i in items)
+
+    SY.dma_start(T.pl[:], T.place[:, :]).then_inc(sem.l_pl, 16)
     SY.dma_start(T.win[:, 0:W], T.ring[:, :]).then_inc(sem.l_ring, 16)
     SY.dma_start(T.land[:, 0:J], T.carry[:, :]).then_inc(sem.l_carry, 16)
     SY.dma_start(T.win[:, W:WX], T.ring[:, 0:WX - W]).then_inc(sem.l_ext, 16)
 
     small = dict(allow_small_or_imprecise_dtypes=True)
     g.iota(T.pcol[:], [[1, 1]], 0, 1).then_inc(sem.io_a, 1)
-    g.iota(T.rmp[:], [[0, 2], [1, 128]], 0, -1, **small).then_inc(sem.io_b, 1)
-    g.iota(T.sraw[:], [[1, 2], [2, 64]], 0, -1, **small).then_inc(sem.io_c, 1)
-    g.iota(T.graw[:], [[8, 8], [0, 8]], 0, 0, **small).then_inc(sem.io_d, 1)
+    g.iota(T.rmp[:], [[0, 2], [1, 128]], 0, -1, **small).then_inc(sem.io_c, 1)
+    g.iota(T.tcol[:], [[-1, RO]], -1, 0, **small).then_inc(sem.io_b, 1)
+    g.iota(T.graw[:], [[8, 8], [0, 8]], 0, 0, **small).then_inc(sem.io_b, 1)
     g.iota(T.ucol[:], [[1, 144]], -16, 0, **small).then_inc(sem.io_d, 1)
-    g.iota(T.tcol[:], [[-1, RO]], -1, 0, **small).then_inc(sem.io_d, 1)
+    g.iota(T.sraw[:], [[1, 2], [2, 64]], 0, -1, **small).then_inc(sem.io_d, 1)
 
     nv = [0]
 
@@ -131,9 +140,7 @@ def rank_program(g, core, T, topo):
     def lcols(c):
         return slice(c * CC, (c + 1) * CC)
 
-    vs(V.memset(T.d0[:], LOW))
     vs(V.memset(T.wl[:], 0.0))
-    vs(V.memset(T.span[:], -2 * M))
     wait(V, "V", "io_a", 1)
     G8, STAGE, ODD, G16, UPPER = (slice(k, k + 1) for k in range(5))
     vs(V.tensor_scalar(T.gi[:, G8], T.pcol[:], 0x70, 1, ALU.bitwise_and, ALU.logical_shift_right))
@@ -141,40 +148,56 @@ def rank_program(g, core, T, topo):
     vs(V.tensor_scalar(T.gi[:, ODD], T.pcol[:], 1, None, ALU.bitwise_and))
     vs(V.tensor_scalar(T.gi[:, G16], T.pcol[:], 0x70, None, ALU.bitwise_and))
     vs(V.tensor_scalar(T.gi[:, UPPER], T.pcol[:], 3, 1, ALU.logical_shift_right, ALU.bitwise_and))
-    wait(V, "V", "io_b", 1)
+    vsync()
+    vs(V.tensor_copy(T.gf[:], T.gi[:]))
+    columns = nv[0]
+    wait(V, "V", "io_c", 1)
     wts(V.tensor_scalar(T.rph[:], T.rmp[:], 0.0, None, ALU.is_equal))
     wts(V.tensor_scalar(T.rn[:], T.rmp[:], 0.0, -1.0, ALU.is_equal, ALU.mult))
     vsync()
-    vs(V.tensor_copy(T.gf[:], T.gi[:]))
-    wts(V.tensor_scalar(T.rp[:], T.rmp[:, 0:128], 0.0, None, ALU.is_equal))
-    wait(V, "V", "io_c", 1)
-    wts(V.tensor_scalar(T.sel[:], T.sraw[:], 0.0, None, ALU.is_equal))
-    vsync()
-    vs(V.tensor_scalar(T.d0[:, 0:EC:S], T.span[:], T.gf[:, ODD], M - 8.0, ALU.mult, ALU.add))
-    vs(V.tensor_scalar(T.cols[:, 0:1], T.gf[:, ODD], -2 * M, M - 0.5, ALU.mult, ALU.add))
-    vs(V.tensor_scalar(T.cols[:, 1:2], T.gf[:, UPPER], -1.0, 1.0, ALU.mult, ALU.add))
+    vs(V.tensor_scalar(T.even[:], T.gf[:, UPPER], -1.0, 1.0, ALU.mult, ALU.add))
     V.tensor_scalar(T.ey[:], T.rmp[:, 0:72], T.gf[:, G8], 0.0, ALU.add, ALU.is_equal).then_inc(sem.plx, 1)
+    wait(V, "V", "io_b", 2)
+
+    def later_stages(slots):
+        for m in slots:
+            wts(V.tensor_scalar(T.wl[:, m, :, m + 1:S], T.graw[:, :, m + 1:S], T.gf[:, G8], None, ALU.is_equal))
+
+    later_stages(range(0, 3))
+    vsync()
     wait(V, "V", "l_pl", 16)
     V.tensor_scalar(T.plx[:, 0:J:2], T.pl[:], -MID, T.gf[:, UPPER], ALU.add, ALU.mult).then_inc(sem.plx, 1)
-    vsync()
-    V.tensor_scalar(T.plx[:, 1:J:2], T.pl[:], -MID, T.cols[:, 1:2], ALU.add, ALU.mult).then_inc(sem.plx, 1)
+    V.tensor_scalar(T.plx[:, 1:J:2], T.pl[:], -MID, T.even[:], ALU.add, ALU.mult).then_inc(sem.plx, 1)
     for c in range(NCH):
         V.tensor_copy(T.off[:, lcols(c)], T.pl[:, lcols(c)]).then_inc(sem["up%d" % c], 1)
-    wait(V, "V", "io_d", 3)
-    vs(V.tensor_scalar(T.kc[:], T.tcol[:], T.gf[:, STAGE], MID, ALU.mult, ALU.add))
-    for m in range(S - 1):
-        wts(V.tensor_scalar(T.wl[:, m, :, m + 1:S], T.graw[:, :, m + 1:S], T.gf[:, G8], None, ALU.is_equal))
+    later_stages(range(3, S - 1))
+
+    na = [0]
+
+    def fill(out, in_, scale, bias):
+        A.activation(out, in_, ACT.Identity, bias=bias, scale=scale).then_inc(sem.sa, 1)
+        na[0] += 1
+
+    wait(A, "A", "io_c", 1)
+    for k in range(0, EC, 256):
+        fill(T.d0[:, k:k + 256], T.rmp[:], 0.0, LOW)
+    wait(A, "A", "vs", columns)
+    fill(T.cols[:, 1:2], T.gf[:, ODD], -2 * M, M - 8.0)
+    fill(T.cols[:, 2:3], T.gf[:, STAGE], -float(RO), MID)
+    fill(T.cols[:, 3:4], T.gf[:, STAGE], -float(RO), MID - LIFT)
+    wait(A, "A", "io_b", 2)
+    A.activation(T.z[:, ZB * NCH:ZB * (NCH + 1), :], T.rmp[:, 0:8 * ZB], ACT.Identity, scale=0.0).then_inc(sem.sb, 1)
+    A.activation(T.cols[:, 0:1], T.gf[:, ODD], ACT.Identity, bias=M - 0.5, scale=-2 * M).then_inc(sem.sb, 1)
+    A.activation(T.kc[:], T.tcol[:], ACT.Identity, bias=MID, scale=T.gf[:, STAGE]).then_inc(sem.sb, 1)
+    wait(A, "A", "sa", na[0])
+    fill(T.d0[:, 0:EC:S], T.rmp[:, 0:JC], 0.0, T.cols[:, 1:2])
+    for h in range(2):
+        fill(T.back[:, h, :], T.rmp[:, 0:CC], 0.0, T.cols[:, 2 + h:3 + h])
+
+    wait(V, "V", "io_d", 2)
     wts(V.tensor_scalar(T.en[:], T.ucol[:, 9:81], T.gf[:, G8], -1.0, ALU.is_equal, ALU.mult))
     wts(V.tensor_scalar(T.ep[:], T.ucol[:, 9:81], T.gf[:, G8], None, ALU.is_equal))
-    vsync()
-    ready = nv[0]
-
-    def late_constants():
-        V.tensor_scalar(T.ed[:], T.ucol[:], T.gf[:, G16], -1.0, ALU.is_equal, ALU.mult).then_inc(sem.late, 1)
-        V.memset(T.z[:, ZB * NCH:ZB * (NCH + 1), :], 0.0).then_inc(sem.late, 1)
-        for h in range(2):
-            V.tensor_scalar(T.back[:, h, :], T.span[:, 0:CC], h * LIFT / (2 * M), T.kc[:, RO - 1:RO],
-                            ALU.mult, ALU.add).then_inc(sem.late, 1)
+    wts(V.tensor_scalar(T.sel[:], T.sraw[:], 0.0, None, ALU.is_equal))
 
     def ring_ready(q, qn, t):
         wait(q, qn, "l_ring", 16)
@@ -230,7 +253,7 @@ def rank_program(g, core, T, topo):
             wait(V, "V", "l_carry", 16)
         else:
             sender = T.cores[(rank - 1 - (t - 1) % (N - 1)) % N]
-            wait(V, "V", "arr%d" % i, neng(sender))
+            wait(V, "V", "arr%d" % i, neng(sender, [i - NCH]))
         s0 = slot_of(T.d1, c, 0)
         V.tensor_tensor_scan(s0, T.land[:, carry_cols(i)], s0, 0.0, ALU.max, ALU.add).then_inc(sem["ins%d" % c], 1)
 
@@ -249,14 +272,37 @@ def rank_program(g, core, T, topo):
                             ).then_inc(sem["up%d" % c], 1)
         else:
             V.tensor_scalar(T.over[:, lcols(c)], places(c), float(W), -float(W), ALU.is_ge, ALU.mult
-                            ).then_inc(sem.ov, 1)
+                            ).then_inc(sem["ov%d" % c], 1)
 
     def wrap(i):
         c = i % NCH
-        wait(V, "V", "ov", c + 1)
+        wait(V, "V", "ov%d" % c, 1)
         V.tensor_tensor(T.ypb[:, lcols(c)], places(c), T.over[:, lcols(c)], ALU.add).then_inc(sem["up%d" % c], 1)
 
+    def direct_selector(i):
+        V.tensor_scalar(T.ed[:], T.ucol[:], T.gf[:, G16], -1.0, ALU.is_equal, ALU.mult).then_inc(sem.ed, 1)
+
+    def own_sum(i):
+        c = i % NCH
+        cols = slice(c * EC, (c + 1) * EC)
+        wait_item(V, "V", "ins", i)
+        V.tensor_tensor_scan(T.ve[:, cols], T.dz[:], T.d1[:, cols], 0.0, ALU.max, ALU.add).then_inc(sem["own%d" % c], 1)
+
+    def own_floor(i):
+        c = i % NCH
+        wait_item(V, "V", "sc", i)
+        V.tensor_scalar(T.vq[:, c * JC:(c + 1) * JC], slot_of(T.fo, c, S - 1), -1.0, T.cols[:, 0:1], ALU.mult, ALU.add
+                        ).then_inc(sem["own%d" % c], 1)
+
+    def own_end(i):
+        c = i % NCH
+        wait(V, "V", "own%d" % c, 2)
+        V.tensor_tensor_scan(T.outc[:, carry_cols(i)], T.vq[:, c * JC:(c + 1) * JC], slot_of(T.ve, c, S - 1), 0.0,
+                             ALU.max, ALU.add).then_inc(sem["ev%d" % c], 1)
+
     def evacuate(i):
+        if i in OWN:
+            return
         wait_item(A, "A", "mc", i)
         A.activation(T.outc[:, carry_cols(i)], ends(i), ACT.Identity, bias=T.cols[:, 0:1]
                      ).then_inc(sem["ev%d" % (i % NCH)], 1)
@@ -274,17 +320,19 @@ def rank_program(g, core, T, topo):
         r0 = 112 if i < NI - NCH else 0
         return buf[:, r0:r0 + 128]
 
-    def mm_slots(i):
+    def mm_slots(i, parts="es"):
         t, c = divmod(i, NCH)
-        wait_item(PE, "P", "ev", i - 2)
-        wait_item(PE, "P", "zo", i - 2)
         gathered(PE, "P", i)
-        for m in range(1, S):
-            PE.matmul(ends(i), turn(T.rph, i), slot_of(T.d1, c, m), m == 1, False)
-        for m in range(1, S - 1):
-            PE.matmul(sums(i), slot_of(T.d1, c, m), T.wl[:, m], m == 1, False)
-        if t > 0 and i < last:
-            PE.matmul(sums(i), T.rph[:, 0:128], moved(c), False, False)
+        if "e" in parts and i not in OWN:
+            wait_item(PE, "P", "ev", i - 2)
+            for m in range(1, S):
+                PE.matmul(ends(i), turn(T.rph, i), slot_of(T.d1, c, m), m == 1, False)
+        if "s" in parts:
+            wait_item(PE, "P", "zo", i - 2)
+            for m in range(1, S - 1):
+                PE.matmul(sums(i), slot_of(T.d1, c, m), T.wl[:, m], m == 1, False)
+            if t > 0 and i < last:
+                PE.matmul(sums(i), T.rph[:, 0:128], moved(c), False, False)
 
     def mm_carry(i, close=False):
         c = i % NCH
@@ -293,10 +341,13 @@ def rank_program(g, core, T, topo):
         ins = PE.matmul(sums(i), T.land[:, carry_cols(i)], T.ep[:, 7:71], False, close)
         if close:
             ins.then_inc(sem["mf%d" % c], 1)
-        PE.matmul(ends(i), turn(T.rph, i), slot_of(T.d1, c, 0), False, False)
+        if i not in OWN:
+            PE.matmul(ends(i), turn(T.rph, i), slot_of(T.d1, c, 0), False, False)
 
     def mm_end(i):
         c = i % NCH
+        if i in OWN:
+            return
         wait_item(PE, "P", "sc", i)
         PE.matmul(ends(i), turn(T.rn, i), slot_of(T.fo, c, S - 1), False, True).then_inc(sem["mc%d" % c], 1)
 
@@ -306,11 +357,14 @@ def rank_program(g, core, T, topo):
             ins = PE.matmul(sums(i), slot_of(T.fo, c, k - 1), T.en[:, 7 - k:71 - k], False, k == S - 1)
         ins.then_inc(sem["mf%d" % c], 1)
 
-    def mm_floors_direct(i):
+    def mm_floors_direct(i, p, stop):
         c = i % NCH
-        for s in range(2 * S):
-            if s % S:
-                PE.matmul(places(c), T.ed[:, 16 - s:144 - s], T.fo[:, c * EC + s - 1:(c + 1) * EC:2 * S], False, False)
+        wait(PE, "P", "ed", 1)
+        wait_item(PE, "P", "sc", i)
+        for s in range(p * S + 1, (p + 1) * S):
+            ins = PE.matmul(places(c), T.ed[:, 16 - s:144 - s], T.fo[:, c * EC + s - 1:(c + 1) * EC:2 * S],
+                            False, stop and s % S == S - 1)
+        return ins
 
     def mm_select(c, b, start, stop):
         PE.matmul(places(c), T.z[:, ZB * b + 1:ZB * b + 17, :], T.sel[:, 0:64], start, False)
@@ -318,9 +372,12 @@ def rank_program(g, core, T, topo):
 
     def mm_back(i):
         c = i % NCH
-        wait(PE, "P", "late", 4)
+        wait(PE, "P", "sa", na[0])
+        wait(PE, "P", "sb", 3)
         wait_item(PE, "P", "up", i)
-        PE.matmul(places(c), T.rp[:], T.back[:, i // last, :], True, False)
+        PE.matmul(places(c), T.rph[:, 0:128], T.back[:, i // last, :], True, False)
+        if i == last:
+            mm_select(c, c, False, False)
 
     def mm_places(i):
         t, c = divmod(i, NCH)
@@ -334,39 +391,35 @@ def rank_program(g, core, T, topo):
         rid, pid, _ = topo.addr(dest(rank, t))
         wait_item(g, "G", "ev", i)
         g.remote_dma(T.land[:, carry_cols(i + NCH)], T.outc[:, carry_cols(i)], sem["arr%d" % (i + NCH)],
-                     sem["sent%d" % t if t < EARLY else "sent"], pid, rid, common(core))
+                     sem["sent%d" % t if t < EARLY else "sent"], pid, rid, engines(core, i))
 
-    first = T.pp0[:, 0:72 * NCH]
     wait(A, "A", "plm", 1)
-    A.activation(T.z[:, 0:ZB * NCH:2, :], first, ACT.Identity).then_inc(sem.plz, 1)
+    A.activation(T.z[:, 0:ZB * NCH:2, :], T.pp0[:, 0:72 * NCH], ACT.Identity).then_inc(sem.plz, 1)
     gather_s(0)
     gather_s(1)
-    wait(A, "A", "vs", ready)
-    for i in range(last):
-        if i + 2 < NI:
-            gather_s(i + 2)
+    wait(A, "A", "sa", na[0])
+    wait(A, "A", "sb", 3)
+    for i in range(NI - NCH):
+        gather_s(i + 2)
         evacuate(i)
         moves(i)
-    wait(A, "A", "late", 4)
-    moves(last)
-    evacuate(last)
+    for k in STAIL.split():
+        {"g": gather_s, "e": evacuate, "m": moves}[k[0]](int(k[1:]))
 
     gather_v(0, 0, VSHARE[0])
-    late_constants()
-    for i in range(NI):
-        v = VSHARE[i + 1] if i < last else 0
-        cut = min(v, VFIRST[i])
-        gather_v(i + 1, 0, cut)
+    wait(V, "V", "sa", na[0])
+    wait(V, "V", "sb", 3)
+    for i in range(last - 2):
+        gather_v(i + 1, 0, VFIRST[i])
         add_carry(i)
-        gather_v(i + 1, cut, v)
+        gather_v(i + 1, VFIRST[i], VSHARE[i + 1])
         if i >= 2:
             lists(i - 2)
         scan(i)
-        if i - 2 >= NI - NCH:
-            wrap(i - 2)
-    for i in (last - 1, last):
-        lists(i)
-        wrap(i)
+    wait(V, "V", "dz", 1)
+    for k in TAIL[3].split():
+        {"a": add_carry, "l": lists, "s": scan, "w": wrap, "x": own_sum, "y": own_floor, "z": own_end,
+         "g": lambda i: gather_v(i, 0, VSHARE[i]), "d": direct_selector}[k[0]](int(k[1:]))
 
     wait(PE, "P", "plx", 3)
     for c in range(NCH):
@@ -374,25 +427,35 @@ def rank_program(g, core, T, topo):
     ins.then_inc(sem.plm, 1)
     wait(PE, "P", "wts", nw[0])
     for i in range(last):
-        mm_slots(i)
-        mm_carry(i)
-        if i - 1 >= NI - NCH:
-            mm_back(i - 1)
-        if i > 0:
-            mm_places(i - 1)
+        for k in OPT[1]:
+            if k in "es":
+                mm_slots(i, k)
+            elif k == "c":
+                mm_carry(i)
+            elif i > 0:
+                mm_places(i - 1)
+        if i + 1 >= NI - NCH:
+            mm_back(i + 1)
         if i == last - 1:
-            mm_slots(last)
-        mm_end(i)
-        mm_floors(i)
+            mm_slots(last, TAIL[0])
+        wait_item(PE, "P", "sc", i)
+        for k in OPT[2]:
+            {"e": mm_end, "f": mm_floors}[k](i)
+    mm_slots(last, TAIL[1])
     mm_carry(last, close=True)
-    mm_back(last - 1)
-    mm_back(last)
-    mm_select(NCH - 1, NCH - 1, False, False)
-    mm_end(last)
-    mm_places(last - 1)
-    mm_floors_direct(last)
-    mm_places(last)
+    for k in TAIL[2]:
+        if k == "p":
+            mm_places(last - 1)
+        elif k == "z":
+            wait_item(PE, "P", "zo", last)
+            ins = mm_select(NCH - 1, NCH, False, TAIL[2][-1] == "z")
+        else:
+            ins = mm_floors_direct(last, int(k), TAIL[2].replace("p", "")[-1] == k)
+        if k == TAIL[2].replace("p", "")[-1]:
+            ins.then_inc(sem["mp%d" % (NCH - 1)], 1)
 
+    wait(g, "G", "sa", na[0])
+    g.affine_select(T.dz[:], T.d0[:], [[0, JC], [1, S]], ALU.is_gt, 0.0, 0, 0).then_inc(sem.dz, 1)
     for i in range(NI - NCH):
         send(i)
 
@@ -407,19 +470,18 @@ def rank_program(g, core, T, topo):
         store(SY, T.yc[112:128, cols], T.outc[0:16, cols])
 
     for t in range(EARLY):
-        wait(SY, "S", "sent%d" % t, NCH * neng(core))
+        wait(SY, "S", "sent%d" % t, neng(core, range(t * NCH, (t + 1) * NCH)))
         store_back(slice(t * J, (t + 1) * J))
-    wait(SY, "S", "sent", (RO - 1 - EARLY) * NCH * neng(core))
+    wait(SY, "S", "sent", neng(core, range(EARLY * NCH, NI - NCH)))
     store_back(slice(EARLY * J, (RO - 1) * J))
-    a, b, e = (RO - 1) * J, RO * J - JC, RO * J
-    for c in range(NCH - 1):
-        wait(SY, "S", "ev%d" % c, RO)
-    store(SY, T.yc[:, a:b], T.outc[:, a:b])
-    for c in range(NCH - 1):
-        wait(SY, "S", "up%d" % c, RO + 1)
-    store(SY, T.yp[:, 0:256 - CC], T.ypb[:, 0:256 - CC])
-    wait(A, "A", "ev%d" % (NCH - 1), RO)
+    a, b, e = (RO - 1) * J, OWN[0] * JC, RO * J
+    for c in range(NCH):
+        wait(A, "A", "ev%d" % c, RO)
+        if c == OWN[0] % NCH - 1:
+            store(A, T.yc[:, a:b], T.outc[:, a:b])
     store(A, T.yc[:, b:e], T.outc[:, b:e])
-    wait(SY, "S", "up%d" % (NCH - 1), RO + 1)
-    store(SY, T.yp[:, 256 - CC:256], T.ypb[:, 256 - CC:256])
+    for h in range(2):
+        for c in (2 * h, 2 * h + 1):
+            wait(SY, "S", "up%d" % c, RO + 1)
+        store(SY, T.yp[:, 2 * h * CC:2 * (h + 1) * CC], T.ypb[:, 2 * h * CC:2 * (h + 1) * CC])
     wait(SY, "S", "st", ns[0])

from concourse.mybir import AluOpType as ALU, ActivationFunctionType as ACT

W, S, J, RO = 4096, 8, 512, 8
NCH = 4
JC = J // NCH
CC = JC * S // 16
EC = JC * S
ZB = 18
MOVE = 240
WX = W + MOVE * (RO - 1)
NI = RO * NCH
M = 3072.0
BIAS = -32.0 + 1.0 / 16
LOW = -32768.0
LIFT = M / 2
MID = 2048.0
VSHARE = [576, 320, 416, 384] + [384, 384, 384, 352] * 6 + [352, 384, 352, 480]
VFIRST = [160] + [0] * 31
EARLY = 2
OPT = ["em", "escp", "ef"]
TAIL = ["s", "", "01pz", "a29 g30 l27 s29 a30 g31 l28 d31 a31 s30 s31 x31 w28 l29 y31 w29 l30 l31 z31 w30 w31"]
STAIL = "g30 e28 m28 g31 e29 m29 e30 m30 m31"
OWN = [NI - 1]

SCRATCH = {
    "win": ("sbuf", [128, WX], "bfloat16"),
    "pl": ("sbuf", [128, 256], "int32"),
    "plx": ("sbuf", [128, J], "float16"),
    "off": ("sbuf", [128, 256], "uint16"),
    "land": ("sbuf", [128, RO * J], "bfloat16"),
    "outc": ("sbuf", [128, RO * J], "bfloat16"),
    "d1": ("sbuf", [128, J * S], "float16"),
    "fo": ("sbuf", [128, J * S], "bfloat16"),
    "d0": ("sbuf", [128, EC], "float16"),
    "dz": ("sbuf", [128, EC], "bfloat16"),
    "ve": ("sbuf", [128, J * S], "float16"),
    "vq": ("sbuf", [128, J], "float16"),
    "z": ("sbuf", [128, ZB * (NCH + 1), 8], "float16"),
    "over": ("sbuf", [128, 256], "float32"),
    "ypb": ("sbuf", [128, 256], "float32"),
    "pcol": ("sbuf", [128, 1], "int32"),
    "gi": ("sbuf", [128, 5], "int32"),
    "gf": ("sbuf", [128, 5], "float32"),
    "cols": ("sbuf", [128, 4], "float32"),
    "rmp": ("sbuf", [128, 256], "bfloat16"),
    "sraw": ("sbuf", [128, 128], "bfloat16"),
    "graw": ("sbuf", [128, 8, 8], "bfloat16"),
    "ucol": ("sbuf", [128, 144], "bfloat16"),
    "tcol": ("sbuf", [128, RO], "float32"),
    "even": ("sbuf", [128, 1], "float32"),
    "rph": ("sbuf", [128, 256], "float16"),
    "rn": ("sbuf", [128, 256], "bfloat16"),
    "sel": ("sbuf", [128, 128], "float16"),
    "en": ("sbuf", [128, 72], "bfloat16"),
    "ep": ("sbuf", [128, 72], "bfloat16"),
    "ed": ("sbuf", [128, 144], "bfloat16"),
    "ey": ("sbuf", [128, 72], "float16"),
    "wl": ("sbuf", [128, S - 1, 8, 8], "float16"),
    "kc": ("sbuf", [128, RO], "float32"),
    "back": ("sbuf", [128, 2, CC], "float16"),
}
for _c in range(NCH):
    SCRATCH["pp%d" % _c] = ("psum", [128, 512], "float32")
for _c in range(2):
    SCRATCH["pc%d" % _c] = ("psum", [128, 512], "float32")
    SCRATCH["po%d" % _c] = ("psum", [128, 512], "float32")

SEMAPHORES = ["l_ring", "l_pl", "l_carry", "l_ext", "io_a", "io_b", "io_c", "io_d", "vs", "wts", "plx", "plm", "plz",
              "sa", "sb", "ed", "st", "sent", "dz", "own"]
for _c in range(NCH):
    SEMAPHORES += ["%s%d" % (_k, _c) for _k in ("ga", "ins", "sc", "mc", "mf", "ev", "zo", "mp", "up", "ov", "own")]
SEMAPHORES += ["arr%d" % _i for _i in range(NCH, NI)] + ["sent%d" % _t for _t in range(RO)]


def rank_program(g, core, T, topo):
    rank = T.rank_of(core)
    if rank is None:
        return
    N = len(T.cores)
    V, A, PE, SY = g.vector, g.scalar, g.tensor, g.sync
    sem = T.sem
    seen = {}
    last = NI - 1

    def wait(q, qn, name, val):
        if val > seen.get((qn, name), 0):
            q.wait_ge(sem[name], val)
            seen[(qn, name)] = val

    def wait_item(q, qn, kind, i):
        if i >= 0:
            wait(q, qn, "%s%d" % (kind, i % NCH), i // NCH + 1)

    def dest(r, t):
        return T.cores[(r + 1 + t % (N - 1)) % N]

    def common(c):
        m = -1
        for o in T.cores:
            if o != c:
                assert topo.may_write(c, o)
                m &= topo.mask(c, o)
        return m

    def engines(c, i):
        e = [k for k in range(common(c).bit_length()) if common(c) >> k & 1]
        return sum(1 << k for k in e)

    def neng(c, items):
        return sum(bin(engines(c, i)).count("1") for i in items)

    SY.dma_start(T.pl[:], T.place[:, :]).then_inc(sem.l_pl, 16)
    SY.dma_start(T.win[:, 0:W], T.ring[:, :]).then_inc(sem.l_ring, 16)
    SY.dma_start(T.land[:, 0:J], T.carry[:, :]).then_inc(sem.l_carry, 16)
    SY.dma_start(T.win[:, W:WX], T.ring[:, 0:WX - W]).then_inc(sem.l_ext, 16)

    small = dict(allow_small_or_imprecise_dtypes=True)
    g.iota(T.pcol[:], [[1, 1]], 0, 1).then_inc(sem.io_a, 1)
    g.iota(T.rmp[:], [[0, 2], [1, 128]], 0, -1, **small).then_inc(sem.io_c, 1)
    g.iota(T.tcol[:], [[-1, RO]], -1, 0, **small).then_inc(sem.io_b, 1)
    g.iota(T.graw[:], [[8, 8], [0, 8]], 0, 0, **small).then_inc(sem.io_b, 1)
    g.iota(T.ucol[:], [[1, 144]], -16, 0, **small).then_inc(sem.io_d, 1)
    g.iota(T.sraw[:], [[1, 2], [2, 64]], 0, -1, **small).then_inc(sem.io_d, 1)

    nv = [0]

    def vs(ins):
        ins.then_inc(sem.vs, 1)
        nv[0] += 1

    def vsync():
        wait(V, "V", "vs", nv[0])

    nw = [0]

    def wts(ins):
        ins.then_inc(sem.wts, 1)
        nw[0] += 1

    def lcols(c):
        return slice(c * CC, (c + 1) * CC)

    vs(V.memset(T.wl[:], 0.0))
    wait(V, "V", "io_a", 1)
    G8, STAGE, ODD, G16, UPPER = (slice(k, k + 1) for k in range(5))
    vs(V.tensor_scalar(T.gi[:, G8], T.pcol[:], 0x70, 1, ALU.bitwise_and, ALU.logical_shift_right))
    vs(V.tensor_scalar(T.gi[:, STAGE], T.pcol[:], S - 1, None, ALU.bitwise_and))
    vs(V.tensor_scalar(T.gi[:, ODD], T.pcol[:], 1, None, ALU.bitwise_and))
    vs(V.tensor_scalar(T.gi[:, G16], T.pcol[:], 0x70, None, ALU.bitwise_and))
    vs(V.tensor_scalar(T.gi[:, UPPER], T.pcol[:], 3, 1, ALU.logical_shift_right, ALU.bitwise_and))
    vsync()
    vs(V.tensor_copy(T.gf[:], T.gi[:]))
    columns = nv[0]
    wait(V, "V", "io_c", 1)
    wts(V.tensor_scalar(T.rph[:], T.rmp[:], 0.0, None, ALU.is_equal))
    wts(V.tensor_scalar(T.rn[:], T.rmp[:], 0.0, -1.0, ALU.is_equal, ALU.mult))
    vsync()
    vs(V.tensor_scalar(T.even[:], T.gf[:, UPPER], -1.0, 1.0, ALU.mult, ALU.add))
    V.tensor_scalar(T.ey[:], T.rmp[:, 0:72], T.gf[:, G8], 0.0, ALU.add, ALU.is_equal).then_inc(sem.plx, 1)
    wait(V, "V", "io_b", 2)

    def later_stages(slots):
        for m in slots:
            wts(V.tensor_scalar(T.wl[:, m, :, m + 1:S], T.graw[:, :, m + 1:S], T.gf[:, G8], None, ALU.is_equal))

    later_stages(range(0, 3))
    vsync()
    wait(V, "V", "l_pl", 16)
    V.tensor_scalar(T.plx[:, 0:J:2], T.pl[:], -MID, T.gf[:, UPPER], ALU.add, ALU.mult).then_inc(sem.plx, 1)
    V.tensor_scalar(T.plx[:, 1:J:2], T.pl[:], -MID, T.even[:], ALU.add, ALU.mult).then_inc(sem.plx, 1)
    for c in range(NCH):
        V.tensor_copy(T.off[:, lcols(c)], T.pl[:, lcols(c)]).then_inc(sem["up%d" % c], 1)
    later_stages(range(3, S - 1))

    na = [0]

    def fill(out, in_, scale, bias):
        A.activation(out, in_, ACT.Identity, bias=bias, scale=scale).then_inc(sem.sa, 1)
        na[0] += 1

    wait(A, "A", "io_c", 1)
    for k in range(0, EC, 256):
        fill(T.d0[:, k:k + 256], T.rmp[:], 0.0, LOW)
    wait(A, "A", "vs", columns)
    fill(T.cols[:, 1:2], T.gf[:, ODD], -2 * M, M - 8.0)
    fill(T.cols[:, 2:3], T.gf[:, STAGE], -float(RO), MID)
    fill(T.cols[:, 3:4], T.gf[:, STAGE], -float(RO), MID - LIFT)
    wait(A, "A", "io_b", 2)
    A.activation(T.z[:, ZB * NCH:ZB * (NCH + 1), :], T.rmp[:, 0:8 * ZB], ACT.Identity, scale=0.0).then_inc(sem.sb, 1)
    A.activation(T.cols[:, 0:1], T.gf[:, ODD], ACT.Identity, bias=M - 0.5, scale=-2 * M).then_inc(sem.sb, 1)
    A.activation(T.kc[:], T.tcol[:], ACT.Identity, bias=MID, scale=T.gf[:, STAGE]).then_inc(sem.sb, 1)
    wait(A, "A", "sa", na[0])
    fill(T.d0[:, 0:EC:S], T.rmp[:, 0:JC], 0.0, T.cols[:, 1:2])
    for h in range(2):
        fill(T.back[:, h, :], T.rmp[:, 0:CC], 0.0, T.cols[:, 2 + h:3 + h])

    wait(V, "V", "io_d", 2)
    wts(V.tensor_scalar(T.en[:], T.ucol[:, 9:81], T.gf[:, G8], -1.0, ALU.is_equal, ALU.mult))
    wts(V.tensor_scalar(T.ep[:], T.ucol[:, 9:81], T.gf[:, G8], None, ALU.is_equal))
    wts(V.tensor_scalar(T.sel[:], T.sraw[:], 0.0, None, ALU.is_equal))

    def ring_ready(q, qn, t):
        wait(q, qn, "l_ring", 16)
        if t > 0:
            wait(q, qn, "l_ext", 16)

    def carry_cols(i):
        return slice(i * JC, (i + 1) * JC)

    def slot_of(buf, c, m):
        return buf[:, c * EC + m:(c + 1) * EC:S]

    def places(c):
        return T["pp%d" % c][:, 0:CC]

    def sums(i):
        return T["po%d" % (i % 2)][:, 0:64]

    def ends(i):
        return T["pc%d" % (i % 2)][:, 0:JC]

    def moved(b):
        return T.z[:, ZB * b + 1:ZB * b + 17:2, :]

    def gather(q, qn, i, a, b):
        t, c = divmod(i, NCH)
        ring_ready(q, qn, t)
        wait_item(q, qn, "up", i)
        src = T.win[:, 0:W + MOVE * t].indirect(T.off[:, c * CC + a // 16:c * CC + b // 16])
        out = T.d1[:, c * EC + a:c * EC + b]
        if q is V:
            ins = V.tensor_scalar(out, src, BIAS, None, ALU.add)
        else:
            ins = A.activation(out, src, ACT.Identity, bias=BIAS)
        ins.then_inc(sem["ga%d" % c], 1)

    def gather_s(i):
        gather(A, "A", i, VSHARE[i], EC)

    def gather_v(i, a, b):
        if a < b:
            gather(V, "V", i, a, b)

    def gathered(q, qn, i):
        calls = [1 + (k == 0) + (k > 0) * ((0 < min(VSHARE[k], VFIRST[k - 1])) + (VFIRST[k - 1] < VSHARE[k]))
                 for k in range(i % NCH, i + 1, NCH)]
        wait(q, qn, "ga%d" % (i % NCH), sum(calls))

    def add_carry(i):
        t, c = divmod(i, NCH)
        gathered(V, "V", i)
        if t == 0:
            wait(V, "V", "l_carry", 16)
        else:
            sender = T.cores[(rank - 1 - (t - 1) % (N - 1)) % N]
            wait(V, "V", "arr%d" % i, neng(sender, [i - NCH]))
        s0 = slot_of(T.d1, c, 0)
        V.tensor_tensor_scan(s0, T.land[:, carry_cols(i)], s0, 0.0, ALU.max, ALU.add).then_inc(sem["ins%d" % c], 1)

    def scan(i):
        c = i % NCH
        cols = slice(c * EC, (c + 1) * EC)
        wait_item(V, "V", "ins", i)
        V.tensor_tensor_scan(T.fo[:, cols], T.d0[:], T.d1[:, cols], LOW, ALU.max, ALU.add
                             ).then_inc(sem["sc%d" % c], 1)

    def lists(i):
        t, c = divmod(i, NCH)
        wait_item(V, "V", "mp", i)
        if t < RO - 1:
            V.tensor_scalar(T.off[:, lcols(c)], places(c), T.kc[:, t:t + 1], None, ALU.add
                            ).then_inc(sem["up%d" % c], 1)
        else:
            V.tensor_scalar(T.over[:, lcols(c)], places(c), float(W), -float(W), ALU.is_ge, ALU.mult
                            ).then_inc(sem["ov%d" % c], 1)

    def wrap(i):
        c = i % NCH
        wait(V, "V", "ov%d" % c, 1)
        V.tensor_tensor(T.ypb[:, lcols(c)], places(c), T.over[:, lcols(c)], ALU.add).then_inc(sem["up%d" % c], 1)

    def direct_selector(i):
        V.tensor_scalar(T.ed[:], T.ucol[:], T.gf[:, G16], -1.0, ALU.is_equal, ALU.mult).then_inc(sem.ed, 1)

    def own_sum(i):
        c = i % NCH
        cols = slice(c * EC, (c + 1) * EC)
        wait_item(V, "V", "ins", i)
        V.tensor_tensor_scan(T.ve[:, cols], T.dz[:], T.d1[:, cols], 0.0, ALU.max, ALU.add).then_inc(sem["own%d" % c], 1)

    def own_floor(i):
        c = i % NCH
        wait_item(V, "V", "sc", i)
        V.tensor_scalar(T.vq[:, c * JC:(c + 1) * JC], slot_of(T.fo, c, S - 1), -1.0, T.cols[:, 0:1], ALU.mult, ALU.add
                        ).then_inc(sem["own%d" % c], 1)

    def own_end(i):
        c = i % NCH
        wait(V, "V", "own%d" % c, 2)
        V.tensor_tensor_scan(T.outc[:, carry_cols(i)], T.vq[:, c * JC:(c + 1) * JC], slot_of(T.ve, c, S - 1), 0.0,
                             ALU.max, ALU.add).then_inc(sem["ev%d" % c], 1)

    def evacuate(i):
        if i in OWN:
            return
        wait_item(A, "A", "mc", i)
        A.activation(T.outc[:, carry_cols(i)], ends(i), ACT.Identity, bias=T.cols[:, 0:1]
                     ).then_inc(sem["ev%d" % (i % NCH)], 1)

    def moves(i):
        c = i % NCH
        wait_item(A, "A", "mf", i)
        if i < last:
            ins = A.activation(moved(c), sums(i), ACT.Identity)
        else:
            ins = A.activation(moved(NCH), sums(i), ACT.Identity, bias=LIFT)
        ins.then_inc(sem["zo%d" % c], 1)

    def turn(buf, i):
        r0 = 112 if i < NI - NCH else 0
        return buf[:, r0:r0 + 128]

    def mm_slots(i, parts="es"):
        t, c = divmod(i, NCH)
        gathered(PE, "P", i)
        if "e" in parts and i not in OWN:
            wait_item(PE, "P", "ev", i - 2)
            for m in range(1, S):
                PE.matmul(ends(i), turn(T.rph, i), slot_of(T.d1, c, m), m == 1, False)
        if "s" in parts:
            wait_item(PE, "P", "zo", i - 2)
            for m in range(1, S - 1):
                PE.matmul(sums(i), slot_of(T.d1, c, m), T.wl[:, m], m == 1, False)
            if t > 0 and i < last:
                PE.matmul(sums(i), T.rph[:, 0:128], moved(c), False, False)

    def mm_carry(i, close=False):
        c = i % NCH
        wait_item(PE, "P", "ins", i)
        PE.matmul(sums(i), slot_of(T.d1, c, 0), T.wl[:, 0], False, False)
        ins = PE.matmul(sums(i), T.land[:, carry_cols(i)], T.ep[:, 7:71], False, close)
        if close:
            ins.then_inc(sem["mf%d" % c], 1)
        if i not in OWN:
            PE.matmul(ends(i), turn(T.rph, i), slot_of(T.d1, c, 0), False, False)

    def mm_end(i):
        c = i % NCH
        if i in OWN:
            return
        wait_item(PE, "P", "sc", i)
        PE.matmul(ends(i), turn(T.rn, i), slot_of(T.fo, c, S - 1), False, True).then_inc(sem["mc%d" % c], 1)

    def mm_floors(i):
        c = i % NCH
        for k in range(1, S):
            ins = PE.matmul(sums(i), slot_of(T.fo, c, k - 1), T.en[:, 7 - k:71 - k], False, k == S - 1)
        ins.then_inc(sem["mf%d" % c], 1)

    def mm_floors_direct(i, p, stop):
        c = i % NCH
        wait(PE, "P", "ed", 1)
        wait_item(PE, "P", "sc", i)
        for s in range(p * S + 1, (p + 1) * S):
            ins = PE.matmul(places(c), T.ed[:, 16 - s:144 - s], T.fo[:, c * EC + s - 1:(c + 1) * EC:2 * S],
                            False, stop and s % S == S - 1)
        return ins

    def mm_select(c, b, start, stop):
        PE.matmul(places(c), T.z[:, ZB * b + 1:ZB * b + 17, :], T.sel[:, 0:64], start, False)
        return PE.matmul(places(c), T.z[:, ZB * b:ZB * b + 16, :], T.sel[:, 64:128], False, stop)

    def mm_back(i):
        c = i % NCH
        wait(PE, "P", "sa", na[0])
        wait(PE, "P", "sb", 3)
        wait_item(PE, "P", "up", i)
        PE.matmul(places(c), T.rph[:, 0:128], T.back[:, i // last, :], True, False)
        if i == last:
            mm_select(c, c, False, False)

    def mm_places(i):
        t, c = divmod(i, NCH)
        wait(PE, "P", "plz", 1)
        wait_item(PE, "P", "up", i)
        wait_item(PE, "P", "zo", i)
        mm_select(c, c if i < last else NCH, t < RO - 1, True).then_inc(sem["mp%d" % c], 1)

    def send(i):
        t = i // NCH
        rid, pid, _ = topo.addr(dest(rank, t))
        wait_item(g, "G", "ev", i)
        g.remote_dma(T.land[:, carry_cols(i + NCH)], T.outc[:, carry_cols(i)], sem["arr%d" % (i + NCH)],
                     sem["sent%d" % t if t < EARLY else "sent"], pid, rid, engines(core, i))

    wait(A, "A", "plm", 1)
    A.activation(T.z[:, 0:ZB * NCH:2, :], T.pp0[:, 0:72 * NCH], ACT.Identity).then_inc(sem.plz, 1)
    gather_s(0)
    gather_s(1)
    wait(A, "A", "sa", na[0])
    wait(A, "A", "sb", 3)
    for i in range(NI - NCH):
        gather_s(i + 2)
        evacuate(i)
        moves(i)
    for k in STAIL.split():
        {"g": gather_s, "e": evacuate, "m": moves}[k[0]](int(k[1:]))

    gather_v(0, 0, VSHARE[0])
    wait(V, "V", "sa", na[0])
    wait(V, "V", "sb", 3)
    for i in range(last - 2):
        gather_v(i + 1, 0, VFIRST[i])
        add_carry(i)
        gather_v(i + 1, VFIRST[i], VSHARE[i + 1])
        if i >= 2:
            lists(i - 2)
        scan(i)
    wait(V, "V", "dz", 1)
    for k in TAIL[3].split():
        {"a": add_carry, "l": lists, "s": scan, "w": wrap, "x": own_sum, "y": own_floor, "z": own_end,
         "g": lambda i: gather_v(i, 0, VSHARE[i]), "d": direct_selector}[k[0]](int(k[1:]))

    wait(PE, "P", "plx", 3)
    for c in range(NCH):
        ins = PE.matmul(T.pp0[:, 72 * c:72 * (c + 1)], T.plx[:, c * JC:(c + 1) * JC], T.ey[:], True, True)
    ins.then_inc(sem.plm, 1)
    wait(PE, "P", "wts", nw[0])
    for i in range(last):
        for k in OPT[1]:
            if k in "es":
                mm_slots(i, k)
            elif k == "c":
                mm_carry(i)
            elif i > 0:
                mm_places(i - 1)
        if i + 1 >= NI - NCH:
            mm_back(i + 1)
        if i == last - 1:
            mm_slots(last, TAIL[0])
        wait_item(PE, "P", "sc", i)
        for k in OPT[2]:
            {"e": mm_end, "f": mm_floors}[k](i)
    mm_slots(last, TAIL[1])
    mm_carry(last, close=True)
    for k in TAIL[2]:
        if k == "p":
            mm_places(last - 1)
        elif k == "z":
            wait_item(PE, "P", "zo", last)
            ins = mm_select(NCH - 1, NCH, False, TAIL[2][-1] == "z")
        else:
            ins = mm_floors_direct(last, int(k), TAIL[2].replace("p", "")[-1] == k)
        if k == TAIL[2].replace("p", "")[-1]:
            ins.then_inc(sem["mp%d" % (NCH - 1)], 1)

    wait(g, "G", "sa", na[0])
    g.affine_select(T.dz[:], T.d0[:], [[0, JC], [1, S]], ALU.is_gt, 0.0, 0, 0).then_inc(sem.dz, 1)
    for i in range(NI - NCH):
        send(i)

    ns = [0]

    def store(q, out, in_):
        q.dma_start(out, in_).then_inc(sem.st, 16)
        ns[0] += 16

    def store_back(cols):
        store(SY, T.yc[0:112, cols], T.outc[16:128, cols])
        store(SY, T.yc[112:128, cols], T.outc[0:16, cols])

    for t in range(EARLY):
        wait(SY, "S", "sent%d" % t, neng(core, range(t * NCH, (t + 1) * NCH)))
        store_back(slice(t * J, (t + 1) * J))
    wait(SY, "S", "sent", neng(core, range(EARLY * NCH, NI - NCH)))
    store_back(slice(EARLY * J, (RO - 1) * J))
    a, b, e = (RO - 1) * J, OWN[0] * JC, RO * J
    for c in range(NCH):
        wait(A, "A", "ev%d" % c, RO)
        if c == OWN[0] % NCH - 1:
            store(A, T.yc[:, a:b], T.outc[:, a:b])
    store(A, T.yc[:, b:e], T.outc[:, b:e])
    for h in range(2):
        for c in (2 * h, 2 * h + 1):
            wait(SY, "S", "up%d" % c, RO + 1)
        store(SY, T.yp[:, 2 * h * CC:2 * (h + 1) * CC], T.ypb[:, 2 * h * CC:2 * (h + 1) * CC])
    wait(SY, "S", "st", ns[0])
